import numpy as np, ml_dtypes
CORES = [48,51,52,55]
N = 4
import mx_ref
BF = ml_dtypes.bfloat16
def gentries(a):
    return np.ascontiguousarray(a.reshape(8, 16, -1).transpose(0, 2, 1)).reshape(8, -1)
def gtable(e):
    e = np.asarray(e); return np.ascontiguousarray(e.reshape(8, -1, 16).transpose(0, 2, 1)).reshape(128, -1).astype(np.int32)
def gcols(t, e):
    v = np.concatenate([t.reshape(8, 16, -1, 4), np.zeros((8, 16, 1, 4), BF)], axis=2)
    return np.ascontiguousarray(np.stack([v[g][:, e[g]] for g in range(8)])).reshape(128, -1)
def gpick(z, e):
    return np.concatenate([z[16 * g:16 * g + 16][:, e[g]] for g in range(8)])
def tile(rs):
    return np.stack(rs, axis=2).reshape(128, -1).astype(BF)
def pick(q, e):
    c = np.concatenate([q[0].reshape(128, -1, 4), np.zeros((128, 1, 4), np.uint8)], axis=1); s = np.concatenate([q[1], np.ones((16, 1), np.uint8)], axis=1)
    return (np.ascontiguousarray(c[:, e].reshape(128, -1)), np.ascontiguousarray(s[:, e]))
def join(*qs):
    return (np.concatenate([q[0] for q in qs], axis=1), np.concatenate([q[1] for q in qs], axis=1))
def put(q, e, v):
    c, s = q[0].reshape(128, -1, 4).copy(), q[1].copy(); c[:, e] = v[0].reshape(128, -1, 4); s[:, e] = v[1]
    return (c.reshape(128, -1), s)
def pk(c, s):
    return (np.ascontiguousarray(c), mx_ref.live(s))
def emit(q):
    return q[0], q[1]
def packed(v, rng):
    q = [mx_ref.quantize(np.ascontiguousarray(v[r])) for r in range(N)]
    return np.stack([a for a, b in q]), np.stack([mx_ref.plane(b, rng) for a, b in q])
def values_of_codes():
    e, c = np.zeros((128, 128, 4), np.float32), np.zeros((128, 2, 4), np.uint8)
    e[np.arange(128), np.arange(128), 0] = 1
    c[:127, :, 0] = np.arange(256).reshape(2, 128).T[:127]
    return mx_ref.matmul(mx_ref.quantize(e.reshape(128, 512).astype(BF)), (c.reshape(128, 8), np.full((16, 2), 127, np.uint8))).T.reshape(-1).astype(np.float64)
CODE_VALUE, SCALE_VALUE = values_of_codes(), 2.0 ** (np.arange(256) - 127.0)
def decode(q):
    return (CODE_VALUE[q[0]].reshape(16, 8, -1, 4) * SCALE_VALUE[q[1]][:, None, :, None] + 0.0).reshape(128, -1).astype(np.float32)
def f(rng, *shape):
    return mx_ref.flush((rng.standard_normal(shape, dtype=np.float32) * np.exp2(rng.integers(-2, 3, shape[:-1] + (1,)))).astype(BF))
def wide(rng, *shape, cols=0):
    v = rng.standard_normal(shape, dtype=np.float32) * np.exp2(rng.integers(-12, 13, shape)).astype(np.float32)
    if cols: v *= np.repeat(np.exp2(rng.integers(-cols, cols + 1, shape[:-2] + (1, shape[-1] // 4))) * (rng.random(shape[:-2] + (1, shape[-1] // 4)) > 0.0625), 4, axis=-1).astype(np.float32)
    return mx_ref.flush(v.astype(BF))
C, B = 384, 192
STEP = [1, 2, 3]
def big(v):
    v = v.astype(np.float32)
    v[np.abs(v) < np.float32(2.0 ** -16)] = 0
    return v.astype(BF)
def numbers_of(rng):
    return {"x": big(f(rng, N, 128, 4 * C)), "u": np.array(f(rng, N, 128, 512)), "v": np.array(f(rng, N, 128, 512))}
def layers(rng):
    k = np.stack([np.exp2(rng.permutation(128) % 5 - 2.0) for r in range(N)])[:, :, None].astype(np.float32)
    return big(rng.standard_normal((N, 128, 2048), dtype=np.float32) * k).reshape(N, 8, 16, 4, 8, 16, 4)
def weights(rng, w):
    c, p = packed(np.ascontiguousarray(w).reshape(N, 128, 2048), rng)
    return {"wc": c, "ws": p}
def still(w, parts):
    for i in parts:
        w[:, :, i] = 0
        w[:, :, :, :, :, i] = 0
    return w
def lists(rng, how, label):
    o, m = np.zeros((N, 8, C), int), np.zeros((N, 8, C), int)
    i = np.arange(B)
    for r in range(N):
        for g in range(8):
            e = rng.permutation(C)
            s, t = [(e[:B], e[B:]), (i, C - 1 - i), (i, B + i), (2 * i, 2 * i + 1), (2 * i + 1, (2 * i + 2) % C), (B + i, B - 1 - i)][how[r, g]]
            j, k = [(rng.permutation(B), rng.permutation(B)), (i, i), (B - 1 - i, B - 1 - i)][label[r, g]]
            o[r, g, s] = j
            o[r, g, t] = B + k
            m[r, g, j] = B + k
            m[r, g, B + k] = j
    return {"o": np.stack([gtable(o[r]) for r in range(N)]), "m": np.stack([gtable(m[r]) for r in range(N)])}
NONE = np.zeros((N, 8), int)
def setup_inputs(rng):
    return {**numbers_of(rng), **lists(rng, NONE, NONE), **weights(rng, layers(rng))}
def setup_inputs_ties(rng):
    d = numbers_of(rng)
    x = d["x"].reshape(N, 8, 16, C, 4)
    x[:, :, 0] = 0
    x[:, :, 0, :, 0] = rng.integers(0, 3, (N, 8, C)).astype(np.float32).astype(BF)
    u = d["u"].reshape(N, 128, 128, 4)
    u[:, :, ::16] = 0
    z = rng.permutation(N)
    for r in range(N):
        for h in range(0, 128, 16): u[r, h, h, 0] = 0.0 if z[r] == 0 else -1.0 if z[r] == 1 else 1.0
    how = (rng.permutation(N)[:, None] + np.arange(8)) % 6
    return {"x": x.reshape(N, 128, 4 * C), "u": u.reshape(N, 128, 512), "v": d["v"], **lists(rng, how, NONE), **weights(rng, still(layers(rng), [0]))}
def setup_inputs_near(rng):
    d = numbers_of(rng)
    x = d["x"].astype(np.float32).reshape(N, 8, 16, C, 4)
    x[:, :, 0] = 0
    x[:, :, 8:] = 0
    u = d["u"].reshape(N, 128, 128, 4)
    u[:, :, ::16] = 0
    z = rng.permutation(N) % 4
    for r in range(N):
        s = rng.integers(0, 16, (8, C))
        c = rng.integers(0, 2, (8, C)) * 2.0 - 1.0
        k = 1.0 if z[r] == 0 else 2.0 ** -30
        if z[r] < 3:
            x[r, :, 0, :, 0] = c if z[r] < 2 else c * (rng.random((8, C)) < 0.25)
            x[r, :, 8] = ((s[:, :, None] >> np.arange(4)) & 1) * np.exp2(np.arange(4) - 23.0)
        else:
            x[r, :, 10, :, 0] = (s % 2) * 1.125 * 2.0 ** -29
            x[r, :, 12, :, 0] = (1 - s % 2) * 2.0 ** -29
        if z[r] < 2: x[r, :, 11, :, 0] = 2.0 ** -10
        for h in range(0, 128, 16):
            if z[r] < 3:
                u[r, h, h, 0] = 1.0 if z[r] == 2 else k
                u[r, h + 8, h] = k
                u[r, h + 11, h, 0] = k
            else:
                u[r, h + 10, h, 0] = 1.125 * k
                u[r, h + 12, h, 0] = 1.25 * k
    return {"x": x.reshape(N, 128, 4 * C).astype(BF), "u": u.reshape(N, 128, 512), "v": d["v"], **lists(rng, NONE, NONE), **weights(rng, still(layers(rng), [0, 8, 9, 10, 11, 12, 13, 14, 15]))}
def setup_inputs_fine(rng):
    d = numbers_of(rng)
    e = rng.integers(8, 15, (N, 8, 16, C, 4))
    e[:, :, 1] = (8 + (np.arange(N)[:, None] + np.arange(8)) % 7)[:, :, None, None]
    x = (1.125 + 0.25 * rng.integers(0, 4, (N, 8, 16, C, 4))) * np.exp2(-e.astype(np.float64))
    x[:, :, ::8, :, 0] = 1.96875
    x *= rng.integers(0, 2, x.shape) * 2.0 - 1.0
    x *= np.exp2(rng.integers(-2, 3, (N, 1, 1, C, 1)).astype(np.float64))
    u = d["u"].reshape(N, 128, 128, 4)
    u[:, :, ::16] = 0
    for h in range(0, 128, 16): u[:, h + 1, h] = 1.0
    w = layers(rng)
    w[:, :, ::8, :, :, :, 0] = 0
    return {"x": x.astype(np.float32).reshape(N, 128, 4 * C).astype(BF), "u": u.reshape(N, 128, 512), "v": d["v"], **lists(rng, NONE, NONE), **weights(rng, w)}
def setup_inputs_ends(rng):
    d = numbers_of(rng)
    z = rng.permutation(N) % 4
    how = np.stack([rng.permutation(np.array([0, 1, 2, 2, 2, 3, 4, 5])) for r in range(N)])
    l = lists(rng, how, np.repeat(1 + z[:, None] % 2, 8, axis=1))
    x = d["x"].reshape(N, 8, 16, C, 4)
    u = d["u"].reshape(N, 128, 128, 4)
    v = d["v"]
    w = layers(rng).reshape(N, 128, 2048)
    for r in range(N):
        c = (1.0 - 2.0 * (np.argsort(gentries(l["o"][r]), axis=1) % 2)) * [2.0 ** 19, -2.0 ** -29, 0.0, 0.0][z[r]]
        if z[r] < 2:
            u[r, :, ::16] = 0
            for h in range(0, 128, 16): u[r, h:h + 16, h] = [2.0 ** 30, 2.0 ** -30][z[r]]
        else:
            k = 5.0 - 2.0 * z[r]
            c = np.full((8, C), k * 2.0 ** 19)
            u[r, :, ::16] = k * 2.0 ** 30
            v[r] = k * 2.0 ** 30
            w[r] = 2.0
        if z[r] == 1: w[r] = 0
        x[r] = c[:, None, :, None].astype(np.float32).astype(BF)
    v = (np.where(v < 0, -1.0, 1.0) * np.where(rng.permutation(N) % 2, 2.0 ** -30, 2.0 ** 30)[:, None, None]).astype(np.float32).astype(BF)
    return {"x": x.reshape(N, 128, 4 * C), "u": u.reshape(N, 128, 512), "v": v, **l, **weights(rng, w)}
def setup_inputs_spread(rng):
    d = setup_inputs(rng)
    d["x"] = big(wide(rng, N, 128, 4 * C, cols=4))
    return d
def check_inputs(d):
    b = []
    for k, lo, hi in (("x", 2.0 ** -29, 2.0 ** 19), ("u", 2.0 ** -30, 2.0 ** 30), ("v", 2.0 ** -30, 2.0 ** 30)):
        a = np.abs(d[k].astype(np.float32))
        if not (np.isfinite(a).all() and ((a == 0) | (a >= lo) & (a <= hi)).all()): b.append("a value of " + k)
    none, least, most = [emit(mx_ref.quantize(np.full((128, 16), k, np.float32).astype(BF)))[1][0, 0] for k in (0.0, 2.0 ** -30, 2.0 ** 30)]
    i = np.arange(C)
    for r in range(N):
        o, m = gentries(d["o"][r]), gentries(d["m"][r])
        if (np.sort(o, axis=1) != i).any(): b.append("o: not every item once")
        if (np.sort(m, axis=1) != i).any() or (np.take_along_axis(m, m, axis=1) != i).any() or (m[:, :B] < B).any(): b.append("m: not mates of births and deaths")
        if ((d["wc"][r] == 0x7F) | (d["wc"][r] == 0xFF)).any(): b.append("wc: a code that is no number")
        s = mx_ref.live(d["ws"][r])
        if ((s != none) & ((s < least) | (s > most))).any(): b.append("ws: a scale out of range")
        elif not (np.sum(np.abs(decode(pk(d["wc"][r], d["ws"][r])).astype(np.float64)).reshape(128, 512, 4), axis=(0, 2)) <= 1024).all(): b.append("W: a column's sum of sizes")
    return b
def of(a, i):
    return np.take_along_axis(a, i, axis=2)
def reference(x, u, v, o, m, wc, ws):
    qu = [mx_ref.quantize(u[r]) for r in range(N)]
    lay = [pk(wc[r], ws[r]) for r in range(N)]
    now = [x[r] for r in range(N)]
    at = np.stack([gentries(o[r]) for r in range(N)])
    mate = np.stack([gentries(m[r]) for r in range(N)])
    for t in range(3):
        k = t % 2
        q = [mx_ref.quantize(now[r]) for r in range(N)]
        held = [decode(q[r]).astype(BF) for r in range(N)]
        s = np.stack([mx_ref.matmul(qu[r], q[r])[::16] for r in range(N)]) + np.float32(0.0)
        place = np.argsort(at, axis=2)
        lo, hi = np.minimum(place, of(place, mate)), np.maximum(place, of(place, mate))
        a, b = at[:, :, k:C - 1:2].copy(), at[:, :, k + 1::2].copy()
        turn = (of(s, a) > of(s, b)) & (of(mate, a) != b)
        nest = (of(lo, a) < of(lo, b)) & (of(hi, b) < of(hi, a)) | (of(lo, b) < of(lo, a)) & (of(hi, a) < of(hi, b))
        switch = turn & nest & ((a < B) == (b < B))
        at2 = at.copy()
        at2[:, :, k:C - 1:2] = np.where(turn, b, a)
        at2[:, :, k + 1::2] = np.where(turn, a, b)
        c = np.zeros((N, 8, C), np.int64) + np.arange(C)
        np.put_along_axis(c, a, np.where(switch, b, a), axis=2)
        np.put_along_axis(c, b, np.where(switch, a, b), axis=2)
        mate2 = of(c, of(mate, c))
        place2 = np.argsort(at2, axis=2)
        gives = of(mate2, at2)[:, :, :B]
        sent = [mx_ref.quantize(gcols(held[r], gives[r])) for r in range(N)]
        met = np.where(place2 < B, place2, B + mate2)
        for r in range(N):
            own = gcols(held[r], mate[r])
            both = np.concatenate([decode(sent[r ^ STEP[t]]).astype(BF), held[r]], axis=1)
            z = mx_ref.quantize(((own.astype(np.float32) + gcols(both, met[r]).astype(np.float32)) * np.float32(0.5)).astype(BF))
            now[r] = tile([gpick(mx_ref.matmul(pick(lay[r], np.arange(128 * i, 128 * i + 128)), z) * np.float32(0.0078125), mate2[r]) + own[:, i::4].astype(np.float32) for i in range(4)])
        at, mate = at2, mate2
    y, om = np.zeros((N, 128, C), np.float32), np.zeros((N, 8, 2 * C), np.float32)
    oc, osc = np.zeros((N, 128, 4 * C), np.uint8), np.zeros((N, 16, C), np.uint8)
    for r in range(N):
        q = mx_ref.quantize(now[r])
        y[r] = mx_ref.matmul(mx_ref.quantize(v[r]), q)
        om[r] = np.concatenate([at[r], mate[r]], axis=1)
        oc[r], osc[r] = emit(q)
    return {"y": y, "om": om, "oc": oc, "osc": osc}

@@ -1,0 +1,477 @@
+from concourse.bass import DstId, RemoteDMATransfer
+from concourse.mybir import dt, AluOpType, ActivationFunctionType
+
+A = AluOpType
+COPY = ActivationFunctionType.Copy
+STEP = (1, 2, 3)
+F8 = "float8_e4m3fn_x4"
+
+SCRATCH = {}
+
+
+def _sb(name, n, d="float32", where="sbuf"):
+    SCRATCH[name] = (where, [128, n], d)
+
+
+for _n, _w in (("X0", 1536), ("UU", 512), ("VV", 512), ("XT", 1536), ("ZT", 1536), ("ET", 768), ("CE", 2048),
+               ("FH", 1536), ("VH", 1536), ("AH", 1536), ("AF", 1536),
+               ("MASK", 576), ("RST", 576), ("TB", 256), ("GF", 576), ("SCF", 576), ("N16", 576)):
+    _sb(_n, _w, "bfloat16")
+for _n, _w in (("qx", 384), ("qz", 384), ("qe", 192), ("qu", 128), ("qv", 128), ("qur", 128), ("qw", 512), ("qce", 512),
+               ("le0", 192), ("le1", 192), ("le2", 192)):
+    _sb(_n, _w, F8)
+    _sb("s" + _n, _w, "uint8")
+for _n, _w in (("SS", 384), ("SGR", 192), ("GB", 1536), ("YS", 384), ("GM", 384), ("SC", 384), ("WT", 64), ("TR", 64),
+               ("TT0", 768), ("TT1", 768), ("TT2", 768), ("OMB", 768), ("PR", 384), ("IOT", 384), ("MN", 384), ("OF", 384),
+               ("OCR", 384), ("RCR", 384), ("IDN", 128), ("DEL", 96), ("TMP", 96), ("QQ", 96)):
+    _sb(_n, _w)
+PART = {}
+
+
+def _parts(buf, d, items):
+    at = 0
+    for n, w in items:
+        PART[n] = (buf, at, w)
+        at += -(-w // 16) * 16
+    _sb(buf, at, d)
+
+
+_parts("FS", "float32", (("DSG", 24), ("NN", 12), ("XX", 48), ("DQ", 48), ("XD", 48), ("NM", 24), ("D0", 24), ("DIS", 12), ("DO", 12), ("KID", 12), ("WM", 12),
+               ("K0", 24), ("K1", 24), ("KC0", 24), ("KC1", 24), ("PQF", 1), ("PQ2", 1), ("P24", 1), ("M15", 1), ("T24", 24),
+               ("PP", 24), ("IDS", 24), ("POSB", 24), ("TD", 24), ("TE", 24), ("SW", 4), ("RW0", 24), ("ITA", 24)))
+for _n, _w in (("OW", 24), ("MW", 24), ("OR", 384), ("MR", 384), ("S0", 96), ("S1", 96), ("S2", 96), ("SN0", 96), ("SN1", 96), ("SN2", 96)):
+    _sb(_n, _w, "int32")
+_parts("IS", "int32", (("KM", 24), ("SM", 24), ("KP", 24), ("TPI", 24), ("DK", 12), ("FK", 12), ("KA", 24), ("KMK", 24), ("WI", 24), ("NB", 24),
+               ("KN", 24), ("DM", 24), ("FM", 24), ("PI", 24), ("PK", 24), ("PS", 24), ("PQI", 1), ("PQ0", 1), ("CKI", 24), ("CKJ", 24)))
+_parts("US", "uint16", (("OL", 24), ("CK", 24), ("N24", 24), ("UL", 8), ("FLL", 36), ("LL", 12), ("RL", 12), ("TPL", 24), ("LM", 24),
+               ("POS", 24), ("ML", 24), ("IL", 24), ("MS", 24), ("OS", 24)))
+for _n in ("P0", "P1", "P2", "P3", "PSC"):
+    _sb(_n, 512, "float32", "psum")
+for _n in ("DD0", "DD1", "DD2"):
+    SCRATCH[_n] = ("dram", [8, 768], "float32")
+SEMAPHORES = ["cv", "ca", "ct", "cp", "re0", "re1", "re2", "ls"] + ["d%d" % k for k in range(60)]
+
+
+def rank_program(g, core, T, topo):
+    rank = T.rank_of(core)
+    if rank is None:
+        return
+    ENG = {"v": g.vector, "a": g.scalar, "t": g.tensor, "p": g, "s": g.sync}
+    cnt, tot, hist, keys = {}, {}, {}, {}
+    known = {q: {} for q in ENG}
+
+    def V(name, lo=0, hi=None, step=1):
+        buf, at, w = PART[name] if name in PART else (name, 0, SCRATCH[name][1][1])
+        return (buf, at + lo, at + (w if hi is None else hi), step)
+
+    def ap(v):
+        return T[v[0]][:, v[1]:v[2]:v[3]] if v[3] > 1 else T[v[0]][:, v[1]:v[2]]
+
+    def by(v):
+        return ap(v).bitcast(dt.uint8)
+
+    def ind(v, l):
+        return ap(v).indirect(ap(l))
+
+    def meet(a, b):
+        if SCRATCH[a[0]][0] == "psum":
+            return True
+        if a[2] <= b[1] or b[2] <= a[1]:
+            return False
+        return not (a[3] == b[3] > 1 and (a[1] - b[1]) % a[3])
+
+    def sem(src):
+        return T.sem["c" + src] if src in ("v", "a", "t", "p") else T.sem[src]
+
+    def wait_for(q, src, c, clk):
+        k = known[q]
+        if k.get(src, 0) >= c:
+            return
+        ENG[q].wait_ge(sem(src), c)
+        k[src] = c
+        for s, x in clk.items():
+            k[s] = max(k.get(s, 0), x)
+
+    def deps(q, rd, wr, skip=()):
+        need = {}
+        for w, vs in ((False, rd), (True, wr)):
+            for v in vs:
+                for e in hist.get(v[0], ()):
+                    if (w or e[0]) and e[2] not in skip and meet(v, e[1]):
+                        c = tot[e[2]] if e[2] in tot else e[3]
+                        if e[2] not in need or need[e[2]][0] < c:
+                            need[e[2]] = (c, e[4])
+        for src in sorted(need, key=lambda s: (s == q, -len(need[s][1]), s)):
+            wait_for(q, src, need[src][0], need[src][1])
+
+    def note(rd, wr, src, c, clk):
+        for v in wr:
+            hist[v[0]] = [e for e in hist.get(v[0], []) if not (src not in tot and v[3] == 1 and v[1] <= e[1][1] and e[1][2] <= v[2])]
+            hist[v[0]].append((True, v, src, c, clk))
+        for v in rd:
+            hist.setdefault(v[0], []).append((False, v, src, c, clk))
+
+    def op(q, rd, wr, emit):
+        deps(q, rd, wr)
+        ins = emit(ENG[q])
+        cnt[q] = cnt.get(q, 0) + 1
+        ins.then_inc(sem(q), 1)
+        note(rd, wr, q, cnt[q], dict(known[q]))
+
+    def dma(q, key, out, in_, rd, wr):
+        if key not in keys:
+            keys[key] = "d%d" % len(keys)
+        k = keys[key]
+        deps(q, rd, wr, skip=[x for y, x in keys.items() if y[:2] == key[:2]])
+        ENG[q].dma_start(out, in_).then_inc(T.sem[k], 16)
+        tot[k] = tot.get(k, 0) + 16
+        note(rd, wr, k, 0, dict(known[q]))
+
+    def tt(out, a, b, f, lst=None):
+        op("v", [a, b] + ([lst] if lst else []), [out],
+           lambda e: e.tensor_tensor(ap(out), ind(a, lst) if lst else ap(a), ap(b), f))
+
+    def ts(out, a, s1, f1, s2=None, f2=None, lst=None, col=None):
+        x = ap(col) if col else s1
+        i = [a] + ([lst] if lst else []) + ([col] if col else [])
+        if f2 is None:
+            op("v", i, [out], lambda e: e.tensor_scalar(ap(out), ind(a, lst) if lst else ap(a), x, None, f1))
+        else:
+            op("v", i, [out], lambda e: e.tensor_scalar(ap(out), ind(a, lst) if lst else ap(a), x, s2, f1, f2))
+
+    def cp(out, a, lst=None):
+        op("v", [a] + ([lst] if lst else []), [out], lambda e: e.tensor_copy(ap(out), ind(a, lst) if lst else ap(a)))
+
+    def act(out, a, scale=1.0, lst=None):
+        op("a", [a] + ([lst] if lst else []), [out],
+           lambda e: e.activation(ap(out), ind(a, lst) if lst else ap(a), COPY, scale=scale))
+
+    def fill(v, c):
+        op("v", [], [v], lambda e: e.memset(ap(v), c))
+
+    def iota(v, pattern, base, ch):
+        op("p", [], [v], lambda e: e.iota(ap(v), pattern, base, ch, allow_small_or_imprecise_dtypes=True))
+
+    def quant(q, n, src, lo=0):
+        c, s = V(q, lo, lo + n), V("s" + q, lo, lo + n)
+        op("v", [src], [c, s], lambda e: e.quantize_mx(ap(c), ap(s), ap(src)))
+
+    def mm(bank, n, l, llo, r):
+        o, a, b = V(bank, 0, n), V(l, llo, llo + 128), V(r, 0, n)
+        c, d = V("s" + l, llo, llo + 128), V("s" + r, 0, n)
+        op("t", [a, b, c, d], [o], lambda e: e.matmul_mx(ap(o), ap(a), ap(c), ap(b), ap(d), True, True))
+
+    def scan(out, a, n):
+        o, x, m = V(out, 0, n), V(a, 0, n), V("RST", 0, n)
+        op("v", [x, m], [o], lambda e: e.tensor_tensor_scan(ap(o), ap(m), ap(x), 0.0, A.mult, A.add))
+
+    def wrapped(src, lst, scr="SC"):
+        tt(V("GM"), src, V("MASK", 0, 384), A.mult, lst)
+        scan(scr, "GM", 384)
+        return V(scr, 15, 384, 16)
+
+    def fld(s, f, side=None):
+        return V(s, f, 96, 4) if side is None else V(s, 48 * side + f, 48 * side + 48, 4)
+
+    dma("s", "ow", T.OW[:], T.o[:], [], [V("OW")])
+    dma("s", "ow", T.MW[:], T.m[:], [], [V("MW")])
+    for q in range(16):
+        dma("sa"[q % 2], "or" + "sa"[q % 2], T.OR[q::16, :], T.o[:], [], [V("OR")])
+    for q in range(16):
+        dma("sa"[q % 2], "mr" + "sa"[q % 2], T.MR[q::16, :], T.m[:], [], [V("MR")])
+    dma("a", "x", T.X0[:], T.x[:], [], [V("X0")])
+    dma("a", "u", T.UU[:], T.u[:], [], [V("UU")])
+    dma("s", "w", T.qw[:].bitcast(dt.uint8), T.wc[:], [], [V("qw")])
+    dma("s", "w", T.sqw[:], T.ws[:], [], [V("sqw")])
+    dma("s", "v", T.VV[:], T.v[:], [], [V("VV")])
+
+    iota(V("PQI"), [[1, 1]], 0, 1)
+    iota(V("K0"), [[1, 2], [32, 12]], 0, 0)
+    iota(V("ITA"), [[1, 24]], 0, 0)
+    iota(V("IOT"), [[1, 384]], 0, 0)
+    iota(V("N16"), [[0, 36], [1, 16]], 0, 0)
+    iota(V("IDN"), [[1, 128]], 0, -1)
+    iota(V("T24"), [[16, 24]], 0, 0)
+    fill(V("CE"), 0.0)
+    fill(V("TB", 192, 256), 0.0)
+    for n in ("WT", "TMP", "XX", "DEL"):
+        fill(V(n), 0.0)
+    ts(V("PQ0"), V("PQI"), 15, A.bitwise_and)
+    cp(V("PQF"), V("PQ0"))
+    ts(V("PQ2"), V("PQF"), 2.0, A.mult)
+    ts(V("P24"), V("PQF"), 24.0, A.mult)
+    ts(V("M15"), V("PQF"), 15.0, A.is_equal)
+    ts(V("K0"), V("K0"), None, A.add, col=V("PQ2"))
+    ts(V("N24"), V("ITA"), None, A.add, col=V("P24"))
+    cp(V("CKI"), V("K0"))
+    ts(V("CKJ"), V("CKI"), 15, A.bitwise_and)
+    ts(V("CKI"), V("CKI"), 4, A.logical_shift_right)
+    ts(V("CKJ"), V("CKJ"), 24, A.mult)
+    tt(V("CKI"), V("CKI"), V("CKJ"), A.add)
+    cp(V("CK"), V("CKI"))
+    ts(V("MASK"), V("N16"), None, A.is_equal, col=V("PQF"))
+    ts(V("RST"), V("N16"), 0.0, A.is_gt)
+    ts(V("KID"), V("T24", 0, 12), None, A.add, col=V("PQF"))
+    cp(V("FLL", 24, 36), V("KID"))
+    ts(V("KC0"), V("K0"), 3072.0, A.add)
+
+    for b in range(4):
+        ts(V("CE", 512 * b + b, 512 * b + 512, 4), V("IDN"), 0.0, A.is_equal)
+    quant("qce", 512, V("CE"))
+
+    cp(V("OL"), V("OW"))
+    op("v", [V("OL"), V("IOT")], [V("PR")], lambda e: e.tensor_copy(ind(V("PR"), V("OL")), ap(V("IOT"))))
+    cp(V("OF"), V("OR"))
+    act(V("OCR"), V("OF"), 1.0, V("CK"))
+    w = wrapped(V("OF"), V("CK"))
+    cp(fld("S0", 2), w)
+    cp(V("OS"), w)
+    cp(V("MN"), V("MR"), V("N24"))
+    w = wrapped(V("MN"), V("OS"))
+    cp(fld("S0", 0), w)
+    cp(V("MS"), w)
+    act(V("RCR"), V("PR"), 512.0, V("MS"))
+    w = wrapped(V("PR"), V("MS"))
+    tt(V("TD"), w, V("K0"), A.is_gt)
+    ts(V("TD"), V("TD"), 1024.0, A.mult)
+    tt(V("RW0"), V("TD"), w, A.add)
+    cp(fld("S0", 1), V("RW0"))
+    ts(V("TE"), fld("S0", 2), 191.5, A.is_gt, 2048.0, A.mult)
+    tt(fld("S0", 3), V("RW0"), V("TE"), A.add)
+    tt(V("OCR"), V("OCR"), V("RCR"), A.add)
+
+    def prep1(t):
+        S = "S%d" % t
+        key = fld(S, 3)
+        if t == 1:
+            ts(V("KP"), key, -1, A.add)
+            key = V("KP")
+        ts(V("KM"), key, 511, A.bitwise_and, 1, A.logical_shift_right)
+        tt(V("DIS"), V("KM", 0, 12), V("KID"), A.is_equal)
+        tt(V("DO"), fld(S, 2, 0), fld(S, 2, 1), A.subtract)
+        cp(V("LL"), fld(S, 2, 0))
+        if t == 1:
+            tt(V("DIS"), V("DIS"), V("WM"), A.max)
+        tt(V("DO"), V("DIS"), V("DO"), A.mult)
+        cp(V("FLL", 0, 24), V("KM"))
+        tt(V("DO"), V("DO"), fld(S, 2, 1), A.add)
+        ts(V("SM"), key, 1, A.bitwise_and)
+        cp(V("RL"), V("DO"))
+        tt(V("DK"), fld(S, 3, 0), fld(S, 3, 1), A.subtract)
+        ts(V("DSG"), V("SM"), -2.0, A.mult, 1.0, A.add)
+        ts(V("FK"), V("DK"), 9, A.arith_shift_right)
+        ts(V("KA"), fld(S, 3), 3072, A.bitwise_and)
+        ts(V("NN"), V("FK"), 0.0, A.not_equal)
+        tt(V("KMK"), V("KC1" if t == 1 else "KC0"), V("KA"), A.subtract)
+        if t == 0:
+            ts(V("TPI"), V("SM"), -192, A.mult, 192, A.add)
+        else:
+            ts(V("TPI"), V("SM"), 191, A.mult, 1 if t == 1 else 0, A.add)
+        if t == 2:
+            ts(V("NB"), fld(S, 3), 511, A.bitwise_and)
+            ts(V("NB"), V("NB"), 1, A.is_equal, 192, A.mult)
+            tt(V("TPI"), V("TPI"), V("NB"), A.add)
+        tt(V("TPI"), V("TPI"), V("KM"), A.add)
+        ts(V("TPL"), V("TPI"), 383, A.min)
+
+    def prep2(t):
+        S = "S%d" % t
+        w = wrapped(V("OCR") if t == 0 else V("TT%d" % (t - 1), 384, 768), V("TPL"))
+        cp(V("WI"), w)
+        ts(V("KN"), V("WI"), 9, A.logical_shift_right)
+        ts(V("NB"), V("WI"), 511, A.bitwise_and)
+        if t == 0:
+            ts(V("TPI"), fld(S, 1), 511, A.bitwise_and)
+            tt(V("D0"), V("TPI"), V("DSG"), A.add)
+            ts(V("TE"), V("NB"), 191.5, A.is_gt, 2048.0, A.mult)
+            tt(V("D0"), V("KN"), V("D0"), A.is_gt)
+            tt(V("TE"), V("TE"), V("KN"), A.add)
+            ts(V("D0"), V("D0"), 1024.0, A.mult)
+            tt(V("KN"), V("TE"), V("D0"), A.add)
+        tt(V("DM"), V("KMK"), V("KN"), A.subtract)
+        tt(V("D0"), V("NB"), fld(S, 0), A.subtract)
+        tt(V("DM"), V("DM"), V("DSG"), A.mult)
+        ts(V("FM"), V("DM"), 9, A.arith_shift_right)
+        ts(V("NM"), V("FM"), 0.0, A.is_equal)
+        tt(fld("DEL", 0), V("NM"), V("D0"), A.mult)
+        tt(V("D0"), V("NM"), V("DSG"), A.mult)
+        tt(fld("DEL", 1), V("DSG"), V("D0"), A.subtract)
+
+    def items(t):
+        cp(V("PI"), V("PP"))
+        src = V("PI")
+        if t == 1:
+            ts(V("PK"), V("PI"), -1, A.add)
+            src = V("PK")
+        ts(V("PS"), src, 1, A.bitwise_and)
+        ts(V("PK"), src, 511, A.bitwise_and, 1, A.logical_shift_right)
+        ts(V("IDS"), V("PS"), -2.0, A.mult, 1.0, A.add)
+        ts(V("POSB"), V("PS"), 96.0, A.mult)
+        cp(V("IL"), V("PK"))
+        tt(V("POSB"), V("POSB"), V("PK"), A.add)
+        ts(V("TD"), V("PK"), 96.0, A.is_ge, 96.0, A.mult)
+        tt(V("POSB"), V("POSB"), V("TD"), A.add)
+
+    def data_lists():
+        quant("qu", 128, V("UU"))
+        cp(V("UL"), V("T24", 0, 8))
+        l = V("UL")
+        op("v", [V("qu"), l], [V("qur")], lambda e: e.tensor_copy(T.qur[:, 0:128].bitcast(dt.uint32), T.qu[:, 0:128].bitcast(dt.uint32).indirect(ap(l))))
+        op("v", [V("squ"), l], [V("squr")], lambda e: e.tensor_copy(T.squr[:, 0:128], T.squ[:, 0:128].indirect(ap(l))))
+
+    prep1(0)
+    cp(V("ML"), V("MW"))
+    quant("qx", 384, V("X0"))
+    data_lists()
+    for t in range(3):
+        S, SN, TT, DD = "S%d" % t, "SN%d" % t, "TT%d" % t, "DD%d" % t
+        dst = T.cores[rank ^ STEP[t]]
+        eng = topo.engines(core, dst)[::2]
+        mask = sum(1 << e for e in eng)
+        rid, pid = topo.addr(dst)[:2]
+        if t:
+            quant("qx", 384, V("XT"))
+        mm("PSC", 384, "qur", 0, "qx")
+        for b in range(4):
+            mm("P%d" % b, 384, "qce", 128 * b, "qx")
+        act(V("SS"), V("PSC", 0, 384))
+        act(V("SGR"), V("SS"), 1.0, V("RL"))
+        for b in range(4):
+            act(V("FH", 384 * b, 384 * b + 384), V("P%d" % b, 0, 384), 0.5)
+        for b in (0, 1):
+            act(V("AH", 384 * b, 384 * b + 384), V("FH", 384 * b, 384 * b + 384), 1.0, V("ML"))
+        prep2(t)
+        tt(V("TB", 0, 192), V("SS"), V("SGR"), A.is_gt, V("LL"))
+        tt(V("GF"), V("TB"), V("MASK"), A.mult, V("FLL"))
+        scan("SCF", "GF", 576)
+        fm, tf = V("SCF", 15, 384, 16), V("SCF", 399, 576, 16)
+        tt(V("XX", 0, 48, 4), tf, V("NN"), A.mult)
+        tt(fld("TMP", 0), fm, fld("DEL", 0), A.mult)
+        tt(fld("TMP", 1), fm, fld("DEL", 1), A.mult)
+        tt(V("XX", 1, 48, 4), tf, V("NN"), A.mult)
+        cp(V("XX", 2, 48, 4), tf)
+        tt(V("QQ"), V("TMP"), V(S), A.add)
+        tt(V("DQ"), V("QQ", 48, 96), V("QQ", 0, 48), A.subtract)
+        tt(V("XD"), V("DQ"), V("XX"), A.mult)
+        tt(V(SN, 0, 48), V("QQ", 0, 48), V("XD"), A.add)
+        tt(V(SN, 48, 96), V("QQ", 48, 96), V("XD"), A.subtract)
+        cp(V("LM", 0, 6), V(SN, 0, 24, 4))
+        cp(V("LM", 6, 12), V(SN, 48, 72, 4))
+        if t == 1:
+            tt(V("SW", 0, 1), V(SN, 92, 93), V(SN, 68, 69), A.subtract)
+            ts(V("SW", 1, 2), V("SW", 0, 1), None, A.mult, col=V("M15"))
+            tt(V("SW", 2, 3), V(SN, 68, 69), V("SW", 1, 2), A.add)
+            cp(V("LM", 11, 12), V("SW", 2, 3))
+        for b in (0, 1):
+            ts(V("ET", b, 768, 4), V("FH", 384 * b, 384 * b + 384), 2.0, A.mult, lst=V("LM", 0, 12))
+        for b in (2, 3):
+            act(V("ET", b, 768, 4), V("FH", 384 * b, 384 * b + 384), 2.0, V("LM", 0, 12))
+        quant("qe", 192, V("ET"))
+        le = "le%d" % t
+        deps("p", [V("qe"), V("sqe")], [])
+        g.remote_dma(by(V(le)), by(V("qe")), T.sem["re%d" % t], T.sem.ls, pid, rid, mask)
+        g.remote_dma(ap(V("s" + le)), ap(V("sqe")), T.sem["re%d" % t], T.sem.ls, pid, rid, mask)
+        tot["ls"] = tot.get("ls", 0) + 2 * len(eng)
+        tot["re%d" % t] = 2 * len(eng)
+        note([V("qe"), V("sqe")], [], "ls", 0, dict(known["p"]))
+        note([], [V(le), V("s" + le)], "re%d" % t, 0, {})
+        cp(V("LM", 12, 18), V(SN, 24, 48, 4))
+        cp(V("LM", 18, 24), V(SN, 72, 96, 4))
+        if t == 1:
+            tt(V("SW", 3, 4), V(SN, 92, 93), V("SW", 1, 2), A.subtract)
+            cp(V("LM", 23, 24), V("SW", 3, 4))
+        for b in range(4):
+            act(V("VH", 384 * b + 192, 384 * b + 384), V("FH", 384 * b, 384 * b + 384), 1.0, V("LM", 12, 24))
+        for b in (2, 3):
+            act(V("AH", 384 * b, 384 * b + 384), V("FH", 384 * b, 384 * b + 384), 1.0, V("ML"))
+        cp(V("WT", 0, 24), V("LM"))
+        if t < 2:
+            ts(V("TE"), fld(SN, 2), 191.5, A.is_gt, 2048.0, A.mult)
+            tt(fld(SN, 3), fld(SN, 1), V("TE"), A.add)
+            ts(V("TD"), fld(SN, 3), 512.0, A.mult)
+            tt(V("WT", 32, 56), V("TD"), fld(SN, 2), A.add)
+        else:
+            cp(V("WT", 32, 56), fld(SN, 2))
+        op("v", [V("WT")], [V("TR")], lambda e: e.transpose(ap(V("TR")), ap(V("WT"))))
+        for a in range(4):
+            for h in range(2):
+                for k in range(2):
+                    dma("s", "dw%d" % t, T[DD][2 * a + h:2 * a + h + 1, 384 * k:384 * k + 384],
+                        T.TR[32 * a:32 * a + 24, 32 * k + 16 * h:32 * k + 16 * h + 16], [V("TR")], [V(DD)])
+        if t < 2:
+            S2, k = "S%d" % (t + 1), "sh%d" % t
+            rs, ws = [V(SN)], [V(S2)]
+            if t == 0:
+                dma("s", k, T[S2][:, 0:48], T[SN][:, 48:96], rs, ws)
+                for i in range(8):
+                    dma("s", k, T[S2][16 * i:16 * i + 15, 48:96], T[SN][16 * i + 1:16 * i + 16, 0:48], rs, ws)
+                dma("s", k, T[S2][15::16, 48:92], T[SN][0::16, 4:48], rs, ws)
+                dma("s", k, T[S2][15::16, 92:96], T[SN][0::16, 0:4], rs, ws)
+            else:
+                dma("s", k, T[S2][:, 48:96], T[SN][:, 0:48], rs, ws)
+                for i in range(8):
+                    dma("s", k, T[S2][16 * i + 1:16 * i + 16, 0:48], T[SN][16 * i:16 * i + 15, 48:96], rs, ws)
+                dma("s", k, T[S2][0::16, 4:48], T[SN][15::16, 48:92], rs, ws)
+                dma("s", k, T[S2][0::16, 0:4], T[SN][15::16, 92:96], rs, ws)
+        for q in range(16):
+            dma("s", "dr%d" % t, T[TT][q::16, :], T[DD][:], [V(DD)], [V(TT)])
+        if t == 0:
+            tt(V("GM"), V("PR"), V("MASK", 0, 384), A.mult)
+            scan("SC", "GM", 384)
+            cp(V("PP"), V("SC", 15, 384, 16))
+        items(t)
+        tt(V("GF", 0, 384), V("TB"), V("MASK", 0, 384), A.mult, V("IL"))
+        scan("SCF", "GF", 384)
+        tt(V("TD"), V("SCF", 15, 384, 16), V("IDS"), A.mult)
+        ts(V("TE"), V("TD"), 96.0, A.mult)
+        tt(V("PP"), V("PP"), V("TD"), A.add)
+        tt(V("POSB"), V("POSB"), V("TE"), A.add)
+        if t == 1:
+            ts(V("TD"), V("PP"), 192.0, A.is_equal, 192.0, A.mult)
+            ts(V("TE"), V("PP"), 0.0, A.is_equal, -256.0, A.mult)
+            tt(V("POSB"), V("POSB"), V("TD"), A.add)
+            tt(V("POSB"), V("POSB"), V("TE"), A.add)
+        cp(V("POS"), V("POSB"))
+        if t == 0:
+            ts(V("D0"), V("K0"), 1.0, A.add)
+            ts(V("DO"), V("D0", 12, 24), 384.0, A.is_equal, -384.0, A.mult)
+            cp(V("K1", 0, 12), V("D0", 0, 12))
+            tt(V("K1", 12, 24), V("D0", 12, 24), V("DO"), A.add)
+            ts(V("KC1"), V("K1"), 3072.0, A.add)
+            ts(V("WM"), V("K1", 0, 12), 383.0, A.is_equal)
+        for b in range(4):
+            mm("P%d" % b, 192, "qce", 128 * b, le)
+        for b in range(4):
+            act(V("VH", 384 * b, 384 * b + 192), V("P%d" % b, 0, 192), 0.5)
+        for b in range(4):
+            v = V("AH", 384 * b, 384 * b + 384)
+            tt(V("ZT", b, 1536, 4), V("VH", 384 * b, 384 * b + 384), v, A.add, V("POS"))
+            act(V("AF", 384 * b, 384 * b + 384), v, 2.0)
+        quant("qz", 384, V("ZT"))
+        for b in range(4):
+            mm("P%d" % b, 384, "qw", 128 * b, "qz")
+            act(V("GB", 384 * b, 384 * b + 384), V("P%d" % b, 0, 384), 0.0078125)
+        if t < 2:
+            prep1(t + 1)
+        else:
+            quant("qv", 128, V("VV"))
+        w = wrapped(V(TT, 0, 384), V("POS"))
+        cp(V("ML"), w)
+        for b in range(4):
+            tt(V("XT", b, 1536, 4), V("GB", 384 * b, 384 * b + 384), V("AF", 384 * b, 384 * b + 384), A.add, V("ML"))
+
+    quant("qx", 384, V("XT"))
+    mm("PSC", 384, "qv", 0, "qx")
+    dma("s", "out", T.oc[:], T.qx[:].bitcast(dt.uint8), [V("qx")], [])
+    for k in range(4):
+        dma("s", "out", T.osc[4 * k:4 * k + 4, :], T.sqx[32 * k:32 * k + 4, :], [V("sqx")], [])
+    act(V("OMB", 0, 384, 2), V("TT2", 384, 576))
+    act(V("OMB", 1, 384, 2), V("TT2", 576, 768))
+    act(V("OMB", 384, 768), V("TT2", 0, 384), 1.0, V("POS"))
+    dma("a", "om", T.om[:], T.OMB[0::16, :], [V("OMB")], [])
+    act(V("YS"), V("PSC", 0, 384))
+    dma("a", "out2", T.y[:], T.YS[:], [V("YS")], [])
+    for k, n in cnt.items():
+        wait_for("p", k, n, {})
+    for k, n in tot.items():
+        wait_for("p", k, n, {})

@@ -1,10 +1,12 @@
-from concourse.bass import DstId, RemoteDMATransfer
+import numpy as np
 from concourse.mybir import dt, AluOpType, ActivationFunctionType
 
 A = AluOpType
 COPY = ActivationFunctionType.Copy
 STEP = (1, 2, 3)
 F8 = "float8_e4m3fn_x4"
+ORDER = {}
+TRIES = 160
 
 SCRATCH = {}
 
@@ -13,38 +15,43 @@ def _sb(name, n, d="float32", where="sbuf"):
     SCRATCH[name] = (where, [128, n], d)
 
 
-for _n, _w in (("X0", 1536), ("UU", 512), ("VV", 512), ("XT", 1536), ("ZT", 1536), ("ET", 768), ("CE", 2048),
-               ("FH", 1536), ("VH", 1536), ("AH", 1536), ("AF", 1536),
-               ("MASK", 576), ("RST", 576), ("TB", 256), ("GF", 576), ("SCF", 576), ("N16", 576)):
+for _n, _w in (("X0", 1536), ("UU", 512), ("VV", 512), ("XT", 1536), ("ZT", 1536), ("ET", 768), ("CE", 2048), ("FH", 1536),
+               ("VH", 1536), ("AH", 1536), ("AF", 1536), ("MASK", 576), ("RST", 576), ("TB", 256), ("N16", 576)):
     _sb(_n, _w, "bfloat16")
 for _n, _w in (("qx", 384), ("qz", 384), ("qe", 192), ("qu", 128), ("qv", 128), ("qur", 128), ("qw", 512), ("qce", 512),
                ("le0", 192), ("le1", 192), ("le2", 192)):
     _sb(_n, _w, F8)
     _sb("s" + _n, _w, "uint8")
-for _n, _w in (("SS", 384), ("SGR", 192), ("GB", 1536), ("YS", 384), ("GM", 384), ("SC", 384), ("WT", 64), ("TR", 64),
-               ("TT0", 768), ("TT1", 768), ("TT2", 768), ("OMB", 768), ("PR", 384), ("IOT", 384), ("MN", 384), ("OF", 384),
-               ("OCR", 384), ("RCR", 384), ("IDN", 128), ("DEL", 96), ("TMP", 96), ("QQ", 96)):
+for _n, _w in (("SS", 384), ("SGR", 192), ("GB", 1536), ("YS", 384), ("WT", 64), ("TR", 64), ("TT0", 768), ("TT1", 768), ("TT2", 768),
+               ("OMB", 768), ("PR", 384), ("IOT", 384), ("MN", 384), ("OF", 384), ("OCR", 384), ("RCR", 384), ("IDN", 128),
+               ("DEL", 96), ("TMP", 96), ("QQ", 96)):
     _sb(_n, _w)
-PART = {}
+for _n, _w in (("OW", 24), ("MW", 24), ("OR", 384), ("MR", 384), ("S0", 96), ("S1", 96), ("S2", 96), ("SN0", 96), ("SN1", 96), ("SN2", 96)):
+    _sb(_n, _w, "int32")
+PART, TOP = {}, {}
 
 
-def _parts(buf, d, items):
+def _parts(buf, d, more, items):
     at = 0
     for n, w in items:
         PART[n] = (buf, at, w)
         at += -(-w // 16) * 16
-    _sb(buf, at, d)
+    TOP[buf] = at
+    _sb(buf, at + more, d)
 
 
-_parts("FS", "float32", (("DSG", 24), ("NN", 12), ("XX", 48), ("DQ", 48), ("XD", 48), ("NM", 24), ("D0", 24), ("DIS", 12), ("DO", 12), ("KID", 12), ("WM", 12),
-               ("K0", 24), ("K1", 24), ("KC0", 24), ("KC1", 24), ("PQF", 1), ("PQ2", 1), ("P24", 1), ("M15", 1), ("T24", 24),
-               ("PP", 24), ("IDS", 24), ("POSB", 24), ("TD", 24), ("TE", 24), ("SW", 4), ("RW0", 24), ("ITA", 24)))
-for _n, _w in (("OW", 24), ("MW", 24), ("OR", 384), ("MR", 384), ("S0", 96), ("S1", 96), ("S2", 96), ("SN0", 96), ("SN1", 96), ("SN2", 96)):
-    _sb(_n, _w, "int32")
-_parts("IS", "int32", (("KM", 24), ("SM", 24), ("KP", 24), ("TPI", 24), ("DK", 12), ("FK", 12), ("KA", 24), ("KMK", 24), ("WI", 24), ("NB", 24),
-               ("KN", 24), ("DM", 24), ("FM", 24), ("PI", 24), ("PK", 24), ("PS", 24), ("PQI", 1), ("PQ0", 1), ("CKI", 24), ("CKJ", 24)))
-_parts("US", "uint16", (("OL", 24), ("CK", 24), ("N24", 24), ("UL", 8), ("FLL", 36), ("LL", 12), ("RL", 12), ("TPL", 24), ("LM", 24),
-               ("POS", 24), ("ML", 24), ("IL", 24), ("MS", 24), ("OS", 24)))
+_parts("GMB", "float32", 8064, (("GM", 384), ("SC", 384)))
+_parts("GFB", "bfloat16", 5760, (("GF", 576), ("SCF", 576), ("GI", 384), ("SCI", 384)))
+_parts("FS", "float32", 4096, (
+    ("DSG", 24), ("NN", 12), ("XX", 48), ("DQ", 48), ("XD", 48), ("NM", 24), ("D0", 24), ("DIS", 12), ("DO", 12), ("KID", 12), ("WM", 12),
+    ("K0", 24), ("K1", 24), ("KC0", 24), ("KC1", 24), ("PQF", 1), ("PQ2", 1), ("P24", 1), ("M15", 1), ("T24", 24), ("IDS", 24),
+    ("POSB", 24), ("TD", 24), ("TE", 24), ("SW", 4), ("RW0", 24), ("ITA", 24)))
+_parts("IS", "int32", 4096, (
+    ("KM", 24), ("SM", 24), ("KP", 24), ("TPI", 24), ("DK", 12), ("FK", 12), ("KA", 24), ("KMK", 24), ("WI", 24), ("NB", 24),
+    ("KN", 24), ("DM", 24), ("FM", 24), ("PP", 24), ("PK", 24), ("PS", 24), ("PQI", 1), ("PQ0", 1), ("CKI", 24), ("CKJ", 24)))
+_parts("US", "uint16", 2048, (
+    ("OL", 24), ("CK", 24), ("N24", 24), ("UL", 8), ("FLL", 36), ("LL", 12), ("RL", 12), ("TPL", 24), ("LM", 24),
+    ("POS", 24), ("ML", 24), ("IL", 24), ("MS", 24), ("OS", 24)))
 for _n in ("P0", "P1", "P2", "P3", "PSC"):
     _sb(_n, 512, "float32", "psum")
 for _n in ("DD0", "DD1", "DD2"):
@@ -57,12 +64,23 @@ def rank_program(g, core, T, topo):
     if rank is None:
         return
     ENG = {"v": g.vector, "a": g.scalar, "t": g.tensor, "p": g, "s": g.sync}
-    cnt, tot, hist, keys = {}, {}, {}, {}
-    known = {q: {} for q in ENG}
+
+    now = dict(PART)
+    top = dict(TOP)
 
     def V(name, lo=0, hi=None, step=1):
-        buf, at, w = PART[name] if name in PART else (name, 0, SCRATCH[name][1][1])
-        return (buf, at + lo, at + (w if hi is None else hi), step)
+        buf, at, w = now[name] if name in now else (name, 0, SCRATCH[name][1][1])
+        hi = w if hi is None else hi
+        return (buf, at + lo, at + hi, step, name if name in now and (lo, hi, step) == (0, w, 1) else None)
+
+    def fresh(v):
+        if v[4] is None:
+            return v
+        buf, at, w = now[v[4]]
+        now[v[4]] = (buf, top[buf], w)
+        top[buf] += -(-w // 16) * 16
+        assert top[buf] <= SCRATCH[buf][1][1]
+        return V(v[4])
 
     def ap(v):
         return T[v[0]][:, v[1]:v[2]:v[3]] if v[3] > 1 else T[v[0]][:, v[1]:v[2]]
@@ -71,7 +89,10 @@ def rank_program(g, core, T, topo):
         return ap(v).bitcast(dt.uint8)
 
     def ind(v, l):
-        return ap(v).indirect(ap(l))
+        return ap(v).indirect(ap(l)) if l else ap(v)
+
+    def width(v):
+        return -(-(v[2] - v[1]) // v[3])
 
     def meet(a, b):
         if SCRATCH[a[0]][0] == "psum":
@@ -80,165 +101,191 @@ def rank_program(g, core, T, topo):
             return False
         return not (a[3] == b[3] > 1 and (a[1] - b[1]) % a[3])
 
-    def sem(src):
-        return T.sem["c" + src] if src in ("v", "a", "t", "p") else T.sem[src]
+    ops, hist = [], {}
 
-    def wait_for(q, src, c, clk):
-        k = known[q]
-        if k.get(src, 0) >= c:
-            return
-        ENG[q].wait_ge(sem(src), c)
-        k[src] = c
-        for s, x in clk.items():
-            k[s] = max(k.get(s, 0), x)
-
-    def deps(q, rd, wr, skip=()):
-        need = {}
+    def add(q, rd, wr, emit, cost, lat=0.0, src=None, n=0):
+        i = len(ops)
+        src = src or q
+        pred = set()
         for w, vs in ((False, rd), (True, wr)):
             for v in vs:
                 for e in hist.get(v[0], ()):
-                    if (w or e[0]) and e[2] not in skip and meet(v, e[1]):
-                        c = tot[e[2]] if e[2] in tot else e[3]
-                        if e[2] not in need or need[e[2]][0] < c:
-                            need[e[2]] = (c, e[4])
-        for src in sorted(need, key=lambda s: (s == q, -len(need[s][1]), s)):
-            wait_for(q, src, need[src][0], need[src][1])
-
-    def note(rd, wr, src, c, clk):
+                    if (w or e[0]) and meet(v, e[1]) and not (src[0] == "d" and ops[e[2]]["src"][:3] == src[:3]):
+                        pred.add(e[2])
+        ops.append({"q": q, "pred": sorted(pred), "emit": emit, "cost": cost, "lat": lat, "src": src, "n": n})
         for v in wr:
-            hist[v[0]] = [e for e in hist.get(v[0], []) if not (src not in tot and v[3] == 1 and v[1] <= e[1][1] and e[1][2] <= v[2])]
-            hist[v[0]].append((True, v, src, c, clk))
+            hist[v[0]] = [e for e in hist.get(v[0], []) if src[0] == "d" or not (v[3] == 1 and v[1] <= e[1][1] and e[1][2] <= v[2])]
+            hist[v[0]].append((True, v, i))
         for v in rd:
-            hist.setdefault(v[0], []).append((False, v, src, c, clk))
+            hist.setdefault(v[0], []).append((False, v, i))
+        return i
 
-    def op(q, rd, wr, emit):
-        deps(q, rd, wr)
-        ins = emit(ENG[q])
-        cnt[q] = cnt.get(q, 0) + 1
-        ins.then_inc(sem(q), 1)
-        note(rd, wr, q, cnt[q], dict(known[q]))
+    CY = 0.00095
+
+    def dve(n, lst, rate=1.0):
+        return 0.05 + 1.5 * CY * n if lst else 0.02 + max(64, rate * n) * CY
+
+    def sb(*vs):
+        return 2.0 if all(SCRATCH[v[0]][0] == "sbuf" for v in vs) else 1.0
 
     def dma(q, key, out, in_, rd, wr):
-        if key not in keys:
-            keys[key] = "d%d" % len(keys)
-        k = keys[key]
-        deps(q, rd, wr, skip=[x for y, x in keys.items() if y[:2] == key[:2]])
-        ENG[q].dma_start(out, in_).then_inc(T.sem[k], 16)
-        tot[k] = tot.get(k, 0) + 16
-        note(rd, wr, k, 0, dict(known[q]))
+        add(q, rd, wr, lambda e: e.dma_start(out, in_), 0.08, 2.4, "d" + key)
 
     def tt(out, a, b, f, lst=None):
-        op("v", [a, b] + ([lst] if lst else []), [out],
-           lambda e: e.tensor_tensor(ap(out), ind(a, lst) if lst else ap(a), ap(b), f))
+        out = fresh(out)
+        add("v", [a, b] + ([lst] if lst else []), [out],
+            lambda e: e.tensor_tensor(ap(out), ind(a, lst), ap(b), f), dve(width(out), lst, sb(a, b)))
 
     def ts(out, a, s1, f1, s2=None, f2=None, lst=None, col=None):
-        x = ap(col) if col else s1
+        out = fresh(out)
         i = [a] + ([lst] if lst else []) + ([col] if col else [])
         if f2 is None:
-            op("v", i, [out], lambda e: e.tensor_scalar(ap(out), ind(a, lst) if lst else ap(a), x, None, f1))
+            add("v", i, [out], lambda e: e.tensor_scalar(ap(out), ind(a, lst), ap(col) if col else s1, None, f1), dve(width(out), lst))
         else:
-            op("v", i, [out], lambda e: e.tensor_scalar(ap(out), ind(a, lst) if lst else ap(a), x, s2, f1, f2))
+            add("v", i, [out], lambda e: e.tensor_scalar(ap(out), ind(a, lst), s1, s2, f1, f2), dve(width(out), lst))
 
     def cp(out, a, lst=None):
-        op("v", [a] + ([lst] if lst else []), [out], lambda e: e.tensor_copy(ap(out), ind(a, lst) if lst else ap(a)))
+        out = fresh(out)
+        add("v", [a] + ([lst] if lst else []), [out], lambda e: e.tensor_copy(ap(out), ind(a, lst)), dve(width(out), lst))
 
     def act(out, a, scale=1.0, lst=None):
-        op("a", [a] + ([lst] if lst else []), [out],
-           lambda e: e.activation(ap(out), ind(a, lst) if lst else ap(a), COPY, scale=scale))
+        add("a", [a] + ([lst] if lst else []), [out],
+            lambda e: e.activation(ap(out), ind(a, lst), COPY, scale=scale), dve(width(out), lst) + 0.02)
 
     def fill(v, c):
-        op("v", [], [v], lambda e: e.memset(ap(v), c))
+        add("v", [], [v], lambda e: e.memset(ap(v), c), dve(width(v), None, 0.5))
 
     def iota(v, pattern, base, ch):
-        op("p", [], [v], lambda e: e.iota(ap(v), pattern, base, ch, allow_small_or_imprecise_dtypes=True))
+        add("p", [], [v], lambda e: e.iota(ap(v), pattern, base, ch, allow_small_or_imprecise_dtypes=True), 0.13 + 2 * CY * width(v))
 
-    def quant(q, n, src, lo=0):
-        c, s = V(q, lo, lo + n), V("s" + q, lo, lo + n)
-        op("v", [src], [c, s], lambda e: e.quantize_mx(ap(c), ap(s), ap(src)))
+    def quant(q, n, src):
+        c, s = V(q, 0, n), V("s" + q, 0, n)
+        add("v", [src], [c, s], lambda e: e.quantize_mx(ap(c), ap(s), ap(src)), 0.03 + 0.0010 * n)
 
     def mm(bank, n, l, llo, r):
         o, a, b = V(bank, 0, n), V(l, llo, llo + 128), V(r, 0, n)
         c, d = V("s" + l, llo, llo + 128), V("s" + r, 0, n)
-        op("t", [a, b, c, d], [o], lambda e: e.matmul_mx(ap(o), ap(a), ap(c), ap(b), ap(d), True, True))
+        add("t", [a, b, c, d], [o], lambda e: e.matmul_mx(ap(o), ap(a), ap(c), ap(b), ap(d), True, True), (n + 16) * 0.0007)
 
     def scan(out, a, n):
-        o, x, m = V(out, 0, n), V(a, 0, n), V("RST", 0, n)
-        op("v", [x, m], [o], lambda e: e.tensor_tensor_scan(ap(o), ap(m), ap(x), 0.0, A.mult, A.add))
+        x, m = V(a, 0, n), V("RST", 0, n)
+        o = fresh(V(out, 0, n))
+        add("v", [x, m], [o], lambda e: e.tensor_tensor_scan(ap(o), ap(m), ap(x), 0.0, A.mult, A.add), dve(n, None, 1.0 if out == "SC" else 0.5))
 
-    def wrapped(src, lst, scr="SC"):
+    def send(t, dst):
+        eng = topo.engines(core, dst)[::2]
+        mask = sum(1 << e for e in eng)
+        rid, pid = topo.addr(dst)[:2]
+        c, s, lc, ls, sem = V("qe"), V("sqe"), V("le%d" % t), V("sle%d" % t), "re%d" % t
+
+        def emit(e):
+            e.remote_dma(by(lc), by(c), T.sem[sem], T.sem.ls, pid, rid, mask)
+            e.remote_dma(ap(ls), ap(s), T.sem[sem], T.sem.ls, pid, rid, mask)
+        i = add("p", [c, s], [], emit, 0.3, 1.0, "ls", 2 * len(eng))
+        j = add("far", [], [lc, ls], None, 0.0, 3.0, sem, 2 * len(eng))
+        ops[j]["pred"].append(i)
+
+    WAKE = 0.12
+
+    def plan(noise, patience):
+        n = len(ops)
+        succ, left = [[] for o in ops], [len(o["pred"]) for o in ops]
+        for i, o in enumerate(ops):
+            for p in o["pred"]:
+                succ[p].append(i)
+        prio = [0.0] * n
+        for i in range(n - 1, -1, -1):
+            prio[i] = ops[i]["cost"] + ops[i]["lat"] + max([prio[j] + WAKE for j in succ[i]] or [0.0])
+        if noise is not None:
+            prio = [p + x for p, x in zip(prio, noise)]
+        free, est, order, end, ready = {}, [0.0] * n, [], 0.0, {}
+        for i in range(n):
+            if not left[i]:
+                ready.setdefault(ops[i]["q"], []).append(i)
+        while True:
+            best = None
+            for q, r in ready.items():
+                if not r:
+                    continue
+                f = free.get(q, 0.0)
+                s = max(f, min(est[i] for i in r))
+                c = max((i for i in r if est[i] <= s), key=lambda i: (prio[i], -i))
+                for i in r:
+                    if prio[i] > prio[c] + 1.0 and est[i] < s + patience * ops[c]["cost"]:
+                        c = i
+                s = max(f, est[c])
+                if best is None or s < best[0]:
+                    best = (s, c, q)
+            if best is None:
+                return end, order
+            s, c, q = best
+            ready[q].remove(c)
+            order.append(c)
+            free[q] = s + ops[c]["cost"]
+            done = free[q] + ops[c]["lat"]
+            end = max(end, done)
+            for j in succ[c]:
+                est[j] = max(est[j], done + WAKE)
+                left[j] -= 1
+                if not left[j]:
+                    ready.setdefault(ops[j]["q"], []).append(j)
+
+    def emit_all():
+        if "order" not in ORDER:
+            rng = np.random.default_rng(7)
+            best = plan(None, 0.3)
+            for k in range(TRIES):
+                x = plan([float(v) for v in rng.normal(0.0, (0.3, 1.0)[k % 2], len(ops))], (0.0, 0.3, 0.7)[k % 3])
+                if x[0] < best[0] - 1e-9:
+                    best = x
+            ORDER["order"], ORDER["end"] = best[1], best[0]
+        known = {q: {} for q in ENG}
+        tot, keys, mark = {}, {}, {}
+        for i in ORDER["order"]:
+            o = ops[i]
+            src, q = o["src"], o["q"]
+            if q not in ENG:
+                keys[src] = T.sem[src]
+                tot[src] = o["n"]
+                mark[i] = (tot[src], {})
+                continue
+            need = {}
+            for p in o["pred"]:
+                s = ops[p]["src"]
+                c, clk = (tot[s] if s[0] == "d" else mark[p][0]), mark[p][1]
+                if s not in need or need[s][0] < c:
+                    need[s] = (c, clk)
+            for s in sorted(need, key=lambda s: (s == q, -len(need[s][1]), s)):
+                if known[q].get(s, 0) < need[s][0]:
+                    ENG[q].wait_ge(keys[s], need[s][0])
+                    known[q][s] = need[s][0]
+                    for y, x in need[s][1].items():
+                        known[q][y] = max(known[q].get(y, 0), x)
+            ins = o["emit"](ENG[q])
+            if src == q:
+                keys[src] = T.sem["c" + q]
+                tot[src] = tot.get(src, 0) + 1
+                ins.then_inc(keys[src], 1)
+            elif src[0] == "d":
+                if src not in keys:
+                    keys[src] = T.sem["d%d" % len(keys)]
+                tot[src] = tot.get(src, 0) + 16
+                ins.then_inc(keys[src], 16)
+            else:
+                keys[src] = T.sem[src]
+                tot[src] = tot.get(src, 0) + o["n"]
+            mark[i] = (tot[src], dict(known[q]))
+        for s, c in tot.items():
+            if known["p"].get(s, 0) < c:
+                g.wait_ge(keys[s], c)
+
+    def wrapped(src, lst):
         tt(V("GM"), src, V("MASK", 0, 384), A.mult, lst)
-        scan(scr, "GM", 384)
-        return V(scr, 15, 384, 16)
+        scan("SC", "GM", 384)
+        return V("SC", 15, 384, 16)
 
     def fld(s, f, side=None):
         return V(s, f, 96, 4) if side is None else V(s, 48 * side + f, 48 * side + 48, 4)
-
-    dma("s", "ow", T.OW[:], T.o[:], [], [V("OW")])
-    dma("s", "ow", T.MW[:], T.m[:], [], [V("MW")])
-    for q in range(16):
-        dma("sa"[q % 2], "or" + "sa"[q % 2], T.OR[q::16, :], T.o[:], [], [V("OR")])
-    for q in range(16):
-        dma("sa"[q % 2], "mr" + "sa"[q % 2], T.MR[q::16, :], T.m[:], [], [V("MR")])
-    dma("a", "x", T.X0[:], T.x[:], [], [V("X0")])
-    dma("a", "u", T.UU[:], T.u[:], [], [V("UU")])
-    dma("s", "w", T.qw[:].bitcast(dt.uint8), T.wc[:], [], [V("qw")])
-    dma("s", "w", T.sqw[:], T.ws[:], [], [V("sqw")])
-    dma("s", "v", T.VV[:], T.v[:], [], [V("VV")])
-
-    iota(V("PQI"), [[1, 1]], 0, 1)
-    iota(V("K0"), [[1, 2], [32, 12]], 0, 0)
-    iota(V("ITA"), [[1, 24]], 0, 0)
-    iota(V("IOT"), [[1, 384]], 0, 0)
-    iota(V("N16"), [[0, 36], [1, 16]], 0, 0)
-    iota(V("IDN"), [[1, 128]], 0, -1)
-    iota(V("T24"), [[16, 24]], 0, 0)
-    fill(V("CE"), 0.0)
-    fill(V("TB", 192, 256), 0.0)
-    for n in ("WT", "TMP", "XX", "DEL"):
-        fill(V(n), 0.0)
-    ts(V("PQ0"), V("PQI"), 15, A.bitwise_and)
-    cp(V("PQF"), V("PQ0"))
-    ts(V("PQ2"), V("PQF"), 2.0, A.mult)
-    ts(V("P24"), V("PQF"), 24.0, A.mult)
-    ts(V("M15"), V("PQF"), 15.0, A.is_equal)
-    ts(V("K0"), V("K0"), None, A.add, col=V("PQ2"))
-    ts(V("N24"), V("ITA"), None, A.add, col=V("P24"))
-    cp(V("CKI"), V("K0"))
-    ts(V("CKJ"), V("CKI"), 15, A.bitwise_and)
-    ts(V("CKI"), V("CKI"), 4, A.logical_shift_right)
-    ts(V("CKJ"), V("CKJ"), 24, A.mult)
-    tt(V("CKI"), V("CKI"), V("CKJ"), A.add)
-    cp(V("CK"), V("CKI"))
-    ts(V("MASK"), V("N16"), None, A.is_equal, col=V("PQF"))
-    ts(V("RST"), V("N16"), 0.0, A.is_gt)
-    ts(V("KID"), V("T24", 0, 12), None, A.add, col=V("PQF"))
-    cp(V("FLL", 24, 36), V("KID"))
-    ts(V("KC0"), V("K0"), 3072.0, A.add)
-
-    for b in range(4):
-        ts(V("CE", 512 * b + b, 512 * b + 512, 4), V("IDN"), 0.0, A.is_equal)
-    quant("qce", 512, V("CE"))
-
-    cp(V("OL"), V("OW"))
-    op("v", [V("OL"), V("IOT")], [V("PR")], lambda e: e.tensor_copy(ind(V("PR"), V("OL")), ap(V("IOT"))))
-    cp(V("OF"), V("OR"))
-    act(V("OCR"), V("OF"), 1.0, V("CK"))
-    w = wrapped(V("OF"), V("CK"))
-    cp(fld("S0", 2), w)
-    cp(V("OS"), w)
-    cp(V("MN"), V("MR"), V("N24"))
-    w = wrapped(V("MN"), V("OS"))
-    cp(fld("S0", 0), w)
-    cp(V("MS"), w)
-    act(V("RCR"), V("PR"), 512.0, V("MS"))
-    w = wrapped(V("PR"), V("MS"))
-    tt(V("TD"), w, V("K0"), A.is_gt)
-    ts(V("TD"), V("TD"), 1024.0, A.mult)
-    tt(V("RW0"), V("TD"), w, A.add)
-    cp(fld("S0", 1), V("RW0"))
-    ts(V("TE"), fld("S0", 2), 191.5, A.is_gt, 2048.0, A.mult)
-    tt(fld("S0", 3), V("RW0"), V("TE"), A.add)
-    tt(V("OCR"), V("OCR"), V("RCR"), A.add)
 
     def prep1(t):
         S = "S%d" % t
@@ -247,31 +294,31 @@ def rank_program(g, core, T, topo):
             ts(V("KP"), key, -1, A.add)
             key = V("KP")
         ts(V("KM"), key, 511, A.bitwise_and, 1, A.logical_shift_right)
+        ts(V("SM"), key, 1, A.bitwise_and)
         tt(V("DIS"), V("KM", 0, 12), V("KID"), A.is_equal)
-        tt(V("DO"), fld(S, 2, 0), fld(S, 2, 1), A.subtract)
-        cp(V("LL"), fld(S, 2, 0))
         if t == 1:
             tt(V("DIS"), V("DIS"), V("WM"), A.max)
+        tt(V("DO"), fld(S, 2, 0), fld(S, 2, 1), A.subtract)
+        cp(V("LL"), fld(S, 2, 0))
         tt(V("DO"), V("DIS"), V("DO"), A.mult)
-        cp(V("FLL", 0, 24), V("KM"))
         tt(V("DO"), V("DO"), fld(S, 2, 1), A.add)
-        ts(V("SM"), key, 1, A.bitwise_and)
         cp(V("RL"), V("DO"))
+        cp(V("FLL", 0, 24), V("KM"))
         tt(V("DK"), fld(S, 3, 0), fld(S, 3, 1), A.subtract)
-        ts(V("DSG"), V("SM"), -2.0, A.mult, 1.0, A.add)
         ts(V("FK"), V("DK"), 9, A.arith_shift_right)
-        ts(V("KA"), fld(S, 3), 3072, A.bitwise_and)
         ts(V("NN"), V("FK"), 0.0, A.not_equal)
+        ts(V("DSG"), V("SM"), -2.0, A.mult, 1.0, A.add)
+        ts(V("KA"), fld(S, 3), 3072, A.bitwise_and)
         tt(V("KMK"), V("KC1" if t == 1 else "KC0"), V("KA"), A.subtract)
         if t == 0:
             ts(V("TPI"), V("SM"), -192, A.mult, 192, A.add)
         else:
             ts(V("TPI"), V("SM"), 191, A.mult, 1 if t == 1 else 0, A.add)
+        tt(V("TPI"), V("TPI"), V("KM"), A.add)
         if t == 2:
             ts(V("NB"), fld(S, 3), 511, A.bitwise_and)
             ts(V("NB"), V("NB"), 1, A.is_equal, 192, A.mult)
             tt(V("TPI"), V("TPI"), V("NB"), A.add)
-        tt(V("TPI"), V("TPI"), V("KM"), A.add)
         ts(V("TPL"), V("TPI"), 383, A.min)
 
     def prep2(t):
@@ -289,48 +336,115 @@ def rank_program(g, core, T, topo):
             ts(V("D0"), V("D0"), 1024.0, A.mult)
             tt(V("KN"), V("TE"), V("D0"), A.add)
         tt(V("DM"), V("KMK"), V("KN"), A.subtract)
-        tt(V("D0"), V("NB"), fld(S, 0), A.subtract)
         tt(V("DM"), V("DM"), V("DSG"), A.mult)
         ts(V("FM"), V("DM"), 9, A.arith_shift_right)
         ts(V("NM"), V("FM"), 0.0, A.is_equal)
+        tt(V("D0"), V("NB"), fld(S, 0), A.subtract)
         tt(fld("DEL", 0), V("NM"), V("D0"), A.mult)
         tt(V("D0"), V("NM"), V("DSG"), A.mult)
         tt(fld("DEL", 1), V("DSG"), V("D0"), A.subtract)
 
     def items(t):
-        cp(V("PI"), V("PP"))
-        src = V("PI")
+        src = V("PP")
         if t == 1:
-            ts(V("PK"), V("PI"), -1, A.add)
+            ts(V("PK"), V("PP"), -1, A.add)
             src = V("PK")
         ts(V("PS"), src, 1, A.bitwise_and)
         ts(V("PK"), src, 511, A.bitwise_and, 1, A.logical_shift_right)
+        cp(V("IL"), V("PK"))
         ts(V("IDS"), V("PS"), -2.0, A.mult, 1.0, A.add)
         ts(V("POSB"), V("PS"), 96.0, A.mult)
-        cp(V("IL"), V("PK"))
         tt(V("POSB"), V("POSB"), V("PK"), A.add)
         ts(V("TD"), V("PK"), 96.0, A.is_ge, 96.0, A.mult)
         tt(V("POSB"), V("POSB"), V("TD"), A.add)
 
-    def data_lists():
-        quant("qu", 128, V("UU"))
-        cp(V("UL"), V("T24", 0, 8))
-        l = V("UL")
-        op("v", [V("qu"), l], [V("qur")], lambda e: e.tensor_copy(T.qur[:, 0:128].bitcast(dt.uint32), T.qu[:, 0:128].bitcast(dt.uint32).indirect(ap(l))))
-        op("v", [V("squ"), l], [V("squr")], lambda e: e.tensor_copy(T.squr[:, 0:128], T.squ[:, 0:128].indirect(ap(l))))
+    dma("s", "ow", T.OW[:], T.o[:], [], [V("OW")])
+    for q in range(16):
+        dma("sa"[q % 2], "or" + "sa"[q % 2], T.OR[q::16, :], T.o[:], [], [V("OR")])
+    for q in range(16):
+        dma("sa"[q % 2], "mr" + "sa"[q % 2], T.MR[q::16, :], T.m[:], [], [V("MR")])
+    dma("s", "mw", T.MW[:], T.m[:], [], [V("MW")])
+    dma("a", "x", T.X0[:], T.x[:], [], [V("X0")])
+    dma("a", "u", T.UU[:], T.u[:], [], [V("UU")])
+    dma("s", "wc", T.qw[:].bitcast(dt.uint8), T.wc[:], [], [V("qw")])
+    dma("s", "ws", T.sqw[:], T.ws[:], [], [V("sqw")])
+    dma("s", "v", T.VV[:], T.v[:], [], [V("VV")])
 
-    prep1(0)
+    iota(V("PQI"), [[1, 1]], 0, 1)
+    iota(V("K0"), [[1, 2], [32, 12]], 0, 0)
+    iota(V("IOT"), [[1, 384]], 0, 0)
+    iota(V("N16"), [[0, 36], [1, 16]], 0, 0)
+    iota(V("ITA"), [[1, 24]], 0, 0)
+    iota(V("IDN"), [[1, 128]], 0, -1)
+    iota(V("T24"), [[16, 24]], 0, 0)
+    fill(V("CE"), 0.0)
+    fill(V("TB", 192, 256), 0.0)
+    for n in ("WT", "TMP", "XX", "DEL"):
+        fill(V(n), 0.0)
+    ts(V("PQ0"), V("PQI"), 15, A.bitwise_and)
+    cp(V("PQF"), V("PQ0"))
+    ts(V("PQ2"), V("PQF"), 2.0, A.mult)
+    ts(V("P24"), V("PQF"), 24.0, A.mult)
+    ts(V("M15"), V("PQF"), 15.0, A.is_equal)
+    ts(V("K0"), V("K0"), None, A.add, col=V("PQ2"))
+    ts(V("N24"), V("ITA"), None, A.add, col=V("P24"))
+    cp(V("CKI"), V("K0"))
+    ts(V("CKJ"), V("CKI"), 15, A.bitwise_and)
+    ts(V("CKJ"), V("CKJ"), 24, A.mult)
+    ts(V("CKI"), V("CKI"), 4, A.logical_shift_right)
+    tt(V("CKI"), V("CKI"), V("CKJ"), A.add)
+    cp(V("CK"), V("CKI"))
+    ts(V("MASK"), V("N16"), None, A.is_equal, col=V("PQF"))
+    ts(V("RST"), V("N16"), 0.0, A.is_gt)
+    ts(V("KID"), V("T24", 0, 12), None, A.add, col=V("PQF"))
+    cp(V("FLL", 24, 36), V("KID"))
+    ts(V("KC0"), V("K0"), 3072.0, A.add)
+    ts(V("TD"), V("K0"), 1.0, A.add)
+    ts(V("DO"), V("TD", 12, 24), 384.0, A.is_equal, -384.0, A.mult)
+    cp(V("K1", 0, 12), V("TD", 0, 12))
+    tt(V("K1", 12, 24), V("TD", 12, 24), V("DO"), A.add)
+    ts(V("KC1"), V("K1"), 3072.0, A.add)
+    ts(V("WM"), V("K1", 0, 12), 383.0, A.is_equal)
+    for b in range(4):
+        ts(V("CE", 512 * b + b, 512 * b + 512, 4), V("IDN"), 0.0, A.is_equal)
+    quant("qce", 512, V("CE"))
+
+    quant("qu", 128, V("UU"))
+    cp(V("UL"), V("T24", 0, 8))
+    ul = V("UL")
+    add("v", [V("qu"), ul], [V("qur")], lambda e: e.tensor_copy(T.qur[:, 0:128].bitcast(dt.uint32), T.qu[:, 0:128].bitcast(dt.uint32).indirect(ap(ul))), 0.25)
+    add("v", [V("squ"), ul], [V("squr")], lambda e: e.tensor_copy(T.squr[:, 0:128], T.squ[:, 0:128].indirect(ap(ul))), 0.25)
+
+    cp(V("OL"), V("OW"))
+    ol = V("OL")
+    add("v", [ol, V("IOT")], [V("PR")], lambda e: e.tensor_copy(ind(V("PR"), ol), ap(V("IOT"))), 1.2)
+    cp(V("OF"), V("OR"))
+    act(V("OCR"), V("OF"), 1.0, V("CK"))
+    w = wrapped(V("OF"), V("CK"))
+    cp(V("OS"), w)
+    cp(fld("S0", 2), w)
+    cp(V("MN"), V("MR"), V("N24"))
+    w = wrapped(V("MN"), V("OS"))
+    cp(V("MS"), w)
+    cp(fld("S0", 0), w)
+    act(V("RCR"), V("PR"), 512.0, V("MS"))
+    w = wrapped(V("PR"), V("MS"))
+    tt(V("TD"), w, V("K0"), A.is_gt)
+    ts(V("TD"), V("TD"), 1024.0, A.mult)
+    tt(V("RW0"), V("TD"), w, A.add)
+    cp(fld("S0", 1), V("RW0"))
+    ts(V("TE"), fld("S0", 2), 191.5, A.is_gt, 2048.0, A.mult)
+    tt(fld("S0", 3), V("RW0"), V("TE"), A.add)
+    tt(V("OCR"), V("OCR"), V("RCR"), A.add)
+    tt(V("GM"), V("PR"), V("MASK", 0, 384), A.mult)
+    scan("SC", "GM", 384)
+    cp(V("PP"), V("SC", 15, 384, 16))
     cp(V("ML"), V("MW"))
-    quant("qx", 384, V("X0"))
-    data_lists()
+    prep1(0)
+
     for t in range(3):
-        S, SN, TT, DD = "S%d" % t, "SN%d" % t, "TT%d" % t, "DD%d" % t
-        dst = T.cores[rank ^ STEP[t]]
-        eng = topo.engines(core, dst)[::2]
-        mask = sum(1 << e for e in eng)
-        rid, pid = topo.addr(dst)[:2]
-        if t:
-            quant("qx", 384, V("XT"))
+        S, SN, TT, DD, le = "S%d" % t, "SN%d" % t, "TT%d" % t, "DD%d" % t, "le%d" % t
+        quant("qx", 384, V("XT" if t else "X0"))
         mm("PSC", 384, "qur", 0, "qx")
         for b in range(4):
             mm("P%d" % b, 384, "qce", 128 * b, "qx")
@@ -338,16 +452,17 @@ def rank_program(g, core, T, topo):
         act(V("SGR"), V("SS"), 1.0, V("RL"))
         for b in range(4):
             act(V("FH", 384 * b, 384 * b + 384), V("P%d" % b, 0, 384), 0.5)
-        for b in (0, 1):
+        for b in range(4):
             act(V("AH", 384 * b, 384 * b + 384), V("FH", 384 * b, 384 * b + 384), 1.0, V("ML"))
         prep2(t)
+        items(t)
         tt(V("TB", 0, 192), V("SS"), V("SGR"), A.is_gt, V("LL"))
         tt(V("GF"), V("TB"), V("MASK"), A.mult, V("FLL"))
         scan("SCF", "GF", 576)
         fm, tf = V("SCF", 15, 384, 16), V("SCF", 399, 576, 16)
-        tt(V("XX", 0, 48, 4), tf, V("NN"), A.mult)
         tt(fld("TMP", 0), fm, fld("DEL", 0), A.mult)
         tt(fld("TMP", 1), fm, fld("DEL", 1), A.mult)
+        tt(V("XX", 0, 48, 4), tf, V("NN"), A.mult)
         tt(V("XX", 1, 48, 4), tf, V("NN"), A.mult)
         cp(V("XX", 2, 48, 4), tf)
         tt(V("QQ"), V("TMP"), V(S), A.add)
@@ -356,34 +471,27 @@ def rank_program(g, core, T, topo):
         tt(V(SN, 0, 48), V("QQ", 0, 48), V("XD"), A.add)
         tt(V(SN, 48, 96), V("QQ", 48, 96), V("XD"), A.subtract)
         cp(V("LM", 0, 6), V(SN, 0, 24, 4))
-        cp(V("LM", 6, 12), V(SN, 48, 72, 4))
         if t == 1:
             tt(V("SW", 0, 1), V(SN, 92, 93), V(SN, 68, 69), A.subtract)
             ts(V("SW", 1, 2), V("SW", 0, 1), None, A.mult, col=V("M15"))
             tt(V("SW", 2, 3), V(SN, 68, 69), V("SW", 1, 2), A.add)
+            tt(V("SW", 3, 4), V(SN, 92, 93), V("SW", 1, 2), A.subtract)
+            cp(V("LM", 6, 11), V(SN, 48, 68, 4))
             cp(V("LM", 11, 12), V("SW", 2, 3))
+            cp(V("LM", 18, 23), V(SN, 72, 92, 4))
+            cp(V("LM", 23, 24), V("SW", 3, 4))
+        else:
+            cp(V("LM", 6, 12), V(SN, 48, 72, 4))
+            cp(V("LM", 18, 24), V(SN, 72, 96, 4))
+        cp(V("LM", 12, 18), V(SN, 24, 48, 4))
         for b in (0, 1):
             ts(V("ET", b, 768, 4), V("FH", 384 * b, 384 * b + 384), 2.0, A.mult, lst=V("LM", 0, 12))
         for b in (2, 3):
             act(V("ET", b, 768, 4), V("FH", 384 * b, 384 * b + 384), 2.0, V("LM", 0, 12))
         quant("qe", 192, V("ET"))
-        le = "le%d" % t
-        deps("p", [V("qe"), V("sqe")], [])
-        g.remote_dma(by(V(le)), by(V("qe")), T.sem["re%d" % t], T.sem.ls, pid, rid, mask)
-        g.remote_dma(ap(V("s" + le)), ap(V("sqe")), T.sem["re%d" % t], T.sem.ls, pid, rid, mask)
-        tot["ls"] = tot.get("ls", 0) + 2 * len(eng)
-        tot["re%d" % t] = 2 * len(eng)
-        note([V("qe"), V("sqe")], [], "ls", 0, dict(known["p"]))
-        note([], [V(le), V("s" + le)], "re%d" % t, 0, {})
-        cp(V("LM", 12, 18), V(SN, 24, 48, 4))
-        cp(V("LM", 18, 24), V(SN, 72, 96, 4))
-        if t == 1:
-            tt(V("SW", 3, 4), V(SN, 92, 93), V("SW", 1, 2), A.subtract)
-            cp(V("LM", 23, 24), V("SW", 3, 4))
+        send(t, T.cores[rank ^ STEP[t]])
         for b in range(4):
             act(V("VH", 384 * b + 192, 384 * b + 384), V("FH", 384 * b, 384 * b + 384), 1.0, V("LM", 12, 24))
-        for b in (2, 3):
-            act(V("AH", 384 * b, 384 * b + 384), V("FH", 384 * b, 384 * b + 384), 1.0, V("ML"))
         cp(V("WT", 0, 24), V("LM"))
         if t < 2:
             ts(V("TE"), fld(SN, 2), 191.5, A.is_gt, 2048.0, A.mult)
@@ -392,12 +500,14 @@ def rank_program(g, core, T, topo):
             tt(V("WT", 32, 56), V("TD"), fld(SN, 2), A.add)
         else:
             cp(V("WT", 32, 56), fld(SN, 2))
-        op("v", [V("WT")], [V("TR")], lambda e: e.transpose(ap(V("TR")), ap(V("WT"))))
+        add("v", [V("WT")], [V("TR")], lambda e: e.transpose(T.TR[:, :], T.WT[:, :]), 0.1)
         for a in range(4):
             for h in range(2):
                 for k in range(2):
                     dma("s", "dw%d" % t, T[DD][2 * a + h:2 * a + h + 1, 384 * k:384 * k + 384],
                         T.TR[32 * a:32 * a + 24, 32 * k + 16 * h:32 * k + 16 * h + 16], [V("TR")], [V(DD)])
+        for q in range(16):
+            dma("s", "dr%d" % t, T[TT][q::16, :], T[DD][:], [V(DD)], [V(TT)])
         if t < 2:
             S2, k = "S%d" % (t + 1), "sh%d" % t
             rs, ws = [V(SN)], [V(S2)]
@@ -413,32 +523,19 @@ def rank_program(g, core, T, topo):
                     dma("s", k, T[S2][16 * i + 1:16 * i + 16, 0:48], T[SN][16 * i:16 * i + 15, 48:96], rs, ws)
                 dma("s", k, T[S2][0::16, 4:48], T[SN][15::16, 48:92], rs, ws)
                 dma("s", k, T[S2][0::16, 0:4], T[SN][15::16, 92:96], rs, ws)
-        for q in range(16):
-            dma("s", "dr%d" % t, T[TT][q::16, :], T[DD][:], [V(DD)], [V(TT)])
-        if t == 0:
-            tt(V("GM"), V("PR"), V("MASK", 0, 384), A.mult)
-            scan("SC", "GM", 384)
-            cp(V("PP"), V("SC", 15, 384, 16))
-        items(t)
-        tt(V("GF", 0, 384), V("TB"), V("MASK", 0, 384), A.mult, V("IL"))
-        scan("SCF", "GF", 384)
-        tt(V("TD"), V("SCF", 15, 384, 16), V("IDS"), A.mult)
+        tt(V("GI"), V("TB"), V("MASK", 0, 384), A.mult, V("IL"))
+        scan("SCI", "GI", 384)
+        tt(V("TD"), V("SCI", 15, 384, 16), V("IDS"), A.mult)
         ts(V("TE"), V("TD"), 96.0, A.mult)
-        tt(V("PP"), V("PP"), V("TD"), A.add)
         tt(V("POSB"), V("POSB"), V("TE"), A.add)
+        if t < 2:
+            tt(V("PP"), V("PP"), V("TD"), A.add)
         if t == 1:
             ts(V("TD"), V("PP"), 192.0, A.is_equal, 192.0, A.mult)
             ts(V("TE"), V("PP"), 0.0, A.is_equal, -256.0, A.mult)
             tt(V("POSB"), V("POSB"), V("TD"), A.add)
             tt(V("POSB"), V("POSB"), V("TE"), A.add)
         cp(V("POS"), V("POSB"))
-        if t == 0:
-            ts(V("D0"), V("K0"), 1.0, A.add)
-            ts(V("DO"), V("D0", 12, 24), 384.0, A.is_equal, -384.0, A.mult)
-            cp(V("K1", 0, 12), V("D0", 0, 12))
-            tt(V("K1", 12, 24), V("D0", 12, 24), V("DO"), A.add)
-            ts(V("KC1"), V("K1"), 3072.0, A.add)
-            ts(V("WM"), V("K1", 0, 12), 383.0, A.is_equal)
         for b in range(4):
             mm("P%d" % b, 192, "qce", 128 * b, le)
         for b in range(4):
@@ -451,27 +548,23 @@ def rank_program(g, core, T, topo):
         for b in range(4):
             mm("P%d" % b, 384, "qw", 128 * b, "qz")
             act(V("GB", 384 * b, 384 * b + 384), V("P%d" % b, 0, 384), 0.0078125)
-        if t < 2:
-            prep1(t + 1)
-        else:
-            quant("qv", 128, V("VV"))
         w = wrapped(V(TT, 0, 384), V("POS"))
         cp(V("ML"), w)
+        if t < 2:
+            prep1(t + 1)
         for b in range(4):
             tt(V("XT", b, 1536, 4), V("GB", 384 * b, 384 * b + 384), V("AF", 384 * b, 384 * b + 384), A.add, V("ML"))
 
+    quant("qv", 128, V("VV"))
     quant("qx", 384, V("XT"))
     mm("PSC", 384, "qv", 0, "qx")
-    dma("s", "out", T.oc[:], T.qx[:].bitcast(dt.uint8), [V("qx")], [])
-    for k in range(4):
-        dma("s", "out", T.osc[4 * k:4 * k + 4, :], T.sqx[32 * k:32 * k + 4, :], [V("sqx")], [])
     act(V("OMB", 0, 384, 2), V("TT2", 384, 576))
     act(V("OMB", 1, 384, 2), V("TT2", 576, 768))
     act(V("OMB", 384, 768), V("TT2", 0, 384), 1.0, V("POS"))
-    dma("a", "om", T.om[:], T.OMB[0::16, :], [V("OMB")], [])
+    dma("s", "om", T.om[:], T.OMB[0::16, :], [V("OMB")], [])
     act(V("YS"), V("PSC", 0, 384))
-    dma("a", "out2", T.y[:], T.YS[:], [V("YS")], [])
-    for k, n in cnt.items():
-        wait_for("p", k, n, {})
-    for k, n in tot.items():
-        wait_for("p", k, n, {})
+    dma("a", "y", T.y[:], T.YS[:], [V("YS")], [])
+    dma("s", "out", T.oc[:], T.qx[:].bitcast(dt.uint8), [V("qx")], [])
+    for k in range(4):
+        dma("s", "out", T.osc[4 * k:4 * k + 4, :], T.sqx[32 * k:32 * k + 4, :], [V("sqx")], [])
+    emit_all()

@@ -6,7 +6,7 @@ COPY = ActivationFunctionType.Copy
 STEP = (1, 2, 3)
 F8 = "float8_e4m3fn_x4"
 ORDER = {}
-TRIES = 160
+TRIES = 1600
 
 SCRATCH = {}
 
@@ -23,7 +23,7 @@ for _n, _w in (("qx", 384), ("qz", 384), ("qe", 192), ("qu", 128), ("qv", 128), 
     _sb(_n, _w, F8)
     _sb("s" + _n, _w, "uint8")
 for _n, _w in (("SS", 384), ("SGR", 192), ("GB", 1536), ("YS", 384), ("WT", 64), ("TR", 64), ("TT0", 768), ("TT1", 768), ("TT2", 768),
-               ("OMB", 768), ("PR", 384), ("IOT", 384), ("MN", 384), ("OF", 384), ("OCR", 384), ("RCR", 384), ("IDN", 128),
+               ("OMB", 768), ("PR", 384), ("IOT", 384), ("MN", 384), ("IW", 384), ("OCR", 384), ("ABI", 128), ("RI", 384), ("TI", 384), ("IDN", 128),
                ("DEL", 96), ("TMP", 96), ("QQ", 96)):
     _sb(_n, _w)
 for _n, _w in (("OW", 24), ("MW", 24), ("OR", 384), ("MR", 384), ("S0", 96), ("S1", 96), ("S2", 96), ("SN0", 96), ("SN1", 96), ("SN2", 96)):
@@ -44,7 +44,7 @@ _parts("GMB", "float32", 8064, (("GM", 384), ("SC", 384)))
 _parts("GFB", "bfloat16", 5760, (("GF", 576), ("SCF", 576), ("GI", 384), ("SCI", 384)))
 _parts("FS", "float32", 4096, (
     ("DSG", 24), ("NN", 12), ("XX", 48), ("DQ", 48), ("XD", 48), ("NM", 24), ("D0", 24), ("DIS", 12), ("DO", 12), ("KID", 12), ("WM", 12),
-    ("K0", 24), ("K1", 24), ("KC0", 24), ("KC1", 24), ("PQF", 1), ("PQ2", 1), ("P24", 1), ("M15", 1), ("T24", 24), ("IDS", 24),
+    ("K0", 24), ("K1", 24), ("KC0", 24), ("KC1", 24), ("PQF", 1), ("PQ2", 1), ("P24", 1), ("M15", 1), ("T24", 24), ("NX", 24), ("PL", 24),
     ("POSB", 24), ("TD", 24), ("TE", 24), ("SW", 4), ("RW0", 24), ("ITA", 24)))
 _parts("IS", "int32", 4096, (
     ("KM", 24), ("SM", 24), ("KP", 24), ("TPI", 24), ("DK", 12), ("FK", 12), ("KA", 24), ("KMK", 24), ("WI", 24), ("NB", 24),
@@ -52,10 +52,10 @@ _parts("IS", "int32", 4096, (
 _parts("US", "uint16", 2048, (
     ("OL", 24), ("CK", 24), ("N24", 24), ("UL", 8), ("FLL", 36), ("LL", 12), ("RL", 12), ("TPL", 24), ("LM", 24),
     ("POS", 24), ("ML", 24), ("IL", 24), ("MS", 24), ("OS", 24)))
-for _n in ("P0", "P1", "P2", "P3", "PSC"):
+for _n in ("P0", "P1", "P2", "P3", "P4", "P5", "P6", "P7"):
     _sb(_n, 512, "float32", "psum")
-for _n in ("DD0", "DD1", "DD2"):
-    SCRATCH[_n] = ("dram", [8, 768], "float32")
+for _n in ("DM0", "DM1", "DM2", "DP0", "DP1", "DP2"):
+    SCRATCH[_n] = ("dram", [8, 384], "float32")
 SEMAPHORES = ["cv", "ca", "ct", "cp", "re0", "re1", "re2", "ls"] + ["d%d" % k for k in range(60)]
 
 
@@ -148,9 +148,9 @@ def rank_program(g, core, T, topo):
         out = fresh(out)
         add("v", [a] + ([lst] if lst else []), [out], lambda e: e.tensor_copy(ap(out), ind(a, lst)), dve(width(out), lst))
 
-    def act(out, a, scale=1.0, lst=None):
+    def act(out, a, scale=1.0, lst=None, func=COPY, bias=0.0):
         add("a", [a] + ([lst] if lst else []), [out],
-            lambda e: e.activation(ap(out), ind(a, lst), COPY, scale=scale), dve(width(out), lst) + 0.02)
+            lambda e: e.activation(ap(out), ind(a, lst), func, **({} if (scale, bias) == (1.0, 0.0) else {"scale": scale, "bias": bias})), dve(width(out), lst) + 0.02)
 
     def fill(v, c):
         add("v", [], [v], lambda e: e.memset(ap(v), c), dve(width(v), None, 0.5))
@@ -158,19 +158,22 @@ def rank_program(g, core, T, topo):
     def iota(v, pattern, base, ch):
         add("p", [], [v], lambda e: e.iota(ap(v), pattern, base, ch, allow_small_or_imprecise_dtypes=True), 0.13 + 2 * CY * width(v))
 
-    def quant(q, n, src):
-        c, s = V(q, 0, n), V("s" + q, 0, n)
+    def quant(q, n, src, lo=0):
+        c, s = V(q, lo, lo + n), V("s" + q, lo, lo + n)
         add("v", [src], [c, s], lambda e: e.quantize_mx(ap(c), ap(s), ap(src)), 0.03 + 0.0010 * n)
 
-    def mm(bank, n, l, llo, r):
-        o, a, b = V(bank, 0, n), V(l, llo, llo + 128), V(r, 0, n)
-        c, d = V("s" + l, llo, llo + 128), V("s" + r, 0, n)
+    def mm(bank, n, l, llo, r, lo=0):
+        o, a, b = V(bank, 0, n), V(l, llo, llo + 128), V(r, lo, lo + n)
+        c, d = V("s" + l, llo, llo + 128), V("s" + r, lo, lo + n)
         add("t", [a, b, c, d], [o], lambda e: e.matmul_mx(ap(o), ap(a), ap(c), ap(b), ap(d), True, True), (n + 16) * 0.0007)
 
     def scan(out, a, n):
         x, m = V(a, 0, n), V("RST", 0, n)
         o = fresh(V(out, 0, n))
         add("v", [x, m], [o], lambda e: e.tensor_tensor_scan(ap(o), ap(m), ap(x), 0.0, A.mult, A.add), dve(n, None, 1.0 if out == "SC" else 0.5))
+
+    def turn32(out, in_):
+        add("v", [in_], [out], lambda e: e.transpose(ap(out), ap(in_)), 0.1)
 
     def send(t, dst):
         eng = topo.engines(core, dst)[::2]
@@ -185,7 +188,7 @@ def rank_program(g, core, T, topo):
         j = add("far", [], [lc, ls], None, 0.0, 3.0, sem, 2 * len(eng))
         ops[j]["pred"].append(i)
 
-    WAKE = 0.12
+    WAKE = 0.17
 
     def plan(noise, patience):
         n = len(ops)
@@ -233,11 +236,19 @@ def rank_program(g, core, T, topo):
     def emit_all():
         if "order" not in ORDER:
             rng = np.random.default_rng(7)
-            best = plan(None, 0.3)
+            best, noise, patience = None, None, 0.3
+            for slope in (0.0, 0.001, 0.002, 0.004):
+                for p in (0.0, 0.3, 0.7):
+                    v = [-slope * i for i in range(len(ops))]
+                    x = plan(v, p)
+                    if best is None or x[0] < best[0]:
+                        best, noise, patience = x, v, p
             for k in range(TRIES):
-                x = plan([float(v) for v in rng.normal(0.0, (0.3, 1.0)[k % 2], len(ops))], (0.0, 0.3, 0.7)[k % 3])
-                if x[0] < best[0] - 1e-9:
-                    best = x
+                f = rng.random(len(ops)) < (0.02, 0.1, 0.4)[k % 3]
+                v = [a + float(b) for a, b in zip(noise, f * rng.normal(0.0, (1.0, 0.5, 0.3)[k % 3], len(ops)))]
+                x = plan(v, patience)
+                if x[0] <= best[0]:
+                    best, noise = x, v
             ORDER["order"], ORDER["end"] = best[1], best[0]
         known = {q: {} for q in ENG}
         tot, keys, mark = {}, {}, {}
@@ -339,10 +350,10 @@ def rank_program(g, core, T, topo):
         tt(V("DM"), V("DM"), V("DSG"), A.mult)
         ts(V("FM"), V("DM"), 9, A.arith_shift_right)
         ts(V("NM"), V("FM"), 0.0, A.is_equal)
+        ts(V("NX"), V("FM"), 0.0, A.not_equal)
         tt(V("D0"), V("NB"), fld(S, 0), A.subtract)
         tt(fld("DEL", 0), V("NM"), V("D0"), A.mult)
-        tt(V("D0"), V("NM"), V("DSG"), A.mult)
-        tt(fld("DEL", 1), V("DSG"), V("D0"), A.subtract)
+        tt(fld("DEL", 1), V("NX"), V("DSG"), A.mult)
 
     def items(t):
         src = V("PP")
@@ -352,11 +363,9 @@ def rank_program(g, core, T, topo):
         ts(V("PS"), src, 1, A.bitwise_and)
         ts(V("PK"), src, 511, A.bitwise_and, 1, A.logical_shift_right)
         cp(V("IL"), V("PK"))
-        ts(V("IDS"), V("PS"), -2.0, A.mult, 1.0, A.add)
-        ts(V("POSB"), V("PS"), 96.0, A.mult)
-        tt(V("POSB"), V("POSB"), V("PK"), A.add)
+        ts(V("PL"), V("PK"), 2, A.mult, t % 2, A.add)
         ts(V("TD"), V("PK"), 96.0, A.is_ge, 96.0, A.mult)
-        tt(V("POSB"), V("POSB"), V("TD"), A.add)
+        tt(V("POSB"), V("PK"), V("TD"), A.add)
 
     dma("s", "ow", T.OW[:], T.o[:], [], [V("OW")])
     for q in range(16):
@@ -377,7 +386,6 @@ def rank_program(g, core, T, topo):
     iota(V("ITA"), [[1, 24]], 0, 0)
     iota(V("IDN"), [[1, 128]], 0, -1)
     iota(V("T24"), [[16, 24]], 0, 0)
-    fill(V("CE"), 0.0)
     fill(V("TB", 192, 256), 0.0)
     for n in ("WT", "TMP", "XX", "DEL"):
         fill(V(n), 0.0)
@@ -395,7 +403,7 @@ def rank_program(g, core, T, topo):
     tt(V("CKI"), V("CKI"), V("CKJ"), A.add)
     cp(V("CK"), V("CKI"))
     ts(V("MASK"), V("N16"), None, A.is_equal, col=V("PQF"))
-    ts(V("RST"), V("N16"), 0.0, A.is_gt)
+    act(V("RST"), V("N16"), func=ActivationFunctionType.Sign)
     ts(V("KID"), V("T24", 0, 12), None, A.add, col=V("PQF"))
     cp(V("FLL", 24, 36), V("KID"))
     ts(V("KC0"), V("K0"), 3072.0, A.add)
@@ -405,50 +413,52 @@ def rank_program(g, core, T, topo):
     tt(V("K1", 12, 24), V("TD", 12, 24), V("DO"), A.add)
     ts(V("KC1"), V("K1"), 3072.0, A.add)
     ts(V("WM"), V("K1", 0, 12), 383.0, A.is_equal)
+    act(V("ABI"), V("IDN"), func=ActivationFunctionType.Abs)
     for b in range(4):
-        ts(V("CE", 512 * b + b, 512 * b + 512, 4), V("IDN"), 0.0, A.is_equal)
+        act(V("CE", 512 * b, 512 * b + 512), V("N16", 0, 512), 0.0)
+        act(V("CE", 512 * b + b, 512 * b + 512, 4), V("ABI"), -1.0, func=ActivationFunctionType.Relu, bias=1.0)
     quant("qce", 512, V("CE"))
 
     quant("qu", 128, V("UU"))
     cp(V("UL"), V("T24", 0, 8))
     ul = V("UL")
     add("v", [V("qu"), ul], [V("qur")], lambda e: e.tensor_copy(T.qur[:, 0:128].bitcast(dt.uint32), T.qu[:, 0:128].bitcast(dt.uint32).indirect(ap(ul))), 0.25)
-    add("v", [V("squ"), ul], [V("squr")], lambda e: e.tensor_copy(T.squr[:, 0:128], T.squ[:, 0:128].indirect(ap(ul))), 0.25)
+    act(V("squr"), V("squ"), lst=ul)
 
     cp(V("OL"), V("OW"))
     ol = V("OL")
     add("v", [ol, V("IOT")], [V("PR")], lambda e: e.tensor_copy(ind(V("PR"), ol), ap(V("IOT"))), 1.2)
-    cp(V("OF"), V("OR"))
-    act(V("OCR"), V("OF"), 1.0, V("CK"))
-    w = wrapped(V("OF"), V("CK"))
+    cp(V("ML"), V("MW"))
+    act(V("RI"), V("PR"), 512.0, V("ML"))
+    cp(V("MN"), V("MR"), V("N24"))
+    tt(V("TI"), V("RI"), V("MN"), A.add)
+    w = wrapped(V("OR"), V("CK"))
     cp(V("OS"), w)
     cp(fld("S0", 2), w)
-    cp(V("MN"), V("MR"), V("N24"))
-    w = wrapped(V("MN"), V("OS"))
-    cp(V("MS"), w)
-    cp(fld("S0", 0), w)
-    act(V("RCR"), V("PR"), 512.0, V("MS"))
-    w = wrapped(V("PR"), V("MS"))
-    tt(V("TD"), w, V("K0"), A.is_gt)
-    ts(V("TD"), V("TD"), 1024.0, A.mult)
-    tt(V("RW0"), V("TD"), w, A.add)
-    cp(fld("S0", 1), V("RW0"))
+    tt(V("IW"), V("RI"), V("IOT"), A.add)
+    act(V("OCR"), V("IW"), 1.0, V("OS"))
+    w = wrapped(V("TI"), V("OS"))
+    cp(V("WI"), w)
+    ts(V("PS"), V("WI"), 9, A.logical_shift_right)
+    ts(fld("S0", 0), V("WI"), 511, A.bitwise_and)
+    tt(V("TD"), V("PS"), V("K0"), A.is_gt)
     ts(V("TE"), fld("S0", 2), 191.5, A.is_gt, 2048.0, A.mult)
-    tt(fld("S0", 3), V("RW0"), V("TE"), A.add)
-    tt(V("OCR"), V("OCR"), V("RCR"), A.add)
+    ts(V("TD"), V("TD"), 1024.0, A.mult)
+    tt(fld("S0", 1), V("TD"), V("PS"), A.add)
+    tt(fld("S0", 3), fld("S0", 1), V("TE"), A.add)
     tt(V("GM"), V("PR"), V("MASK", 0, 384), A.mult)
     scan("SC", "GM", 384)
     cp(V("PP"), V("SC", 15, 384, 16))
-    cp(V("ML"), V("MW"))
     prep1(0)
 
     for t in range(3):
-        S, SN, TT, DD, le = "S%d" % t, "SN%d" % t, "TT%d" % t, "DD%d" % t, "le%d" % t
-        quant("qx", 384, V("XT" if t else "X0"))
-        mm("PSC", 384, "qur", 0, "qx")
+        S, SN, TT, le = "S%d" % t, "SN%d" % t, "TT%d" % t, "le%d" % t
+        for h in range(2):
+            quant("qx", 192, V("XT" if t else "X0", 768 * h, 768 * h + 768), 192 * h)
+            mm("P%d" % (4 + h), 192, "qur", 0, "qx", 192 * h)
+            act(V("SS", 192 * h, 192 * h + 192), V("P%d" % (4 + h), 0, 192))
         for b in range(4):
             mm("P%d" % b, 384, "qce", 128 * b, "qx")
-        act(V("SS"), V("PSC", 0, 384))
         act(V("SGR"), V("SS"), 1.0, V("RL"))
         for b in range(4):
             act(V("FH", 384 * b, 384 * b + 384), V("P%d" % b, 0, 384), 0.5)
@@ -500,14 +510,15 @@ def rank_program(g, core, T, topo):
             tt(V("WT", 32, 56), V("TD"), fld(SN, 2), A.add)
         else:
             cp(V("WT", 32, 56), fld(SN, 2))
-        add("v", [V("WT")], [V("TR")], lambda e: e.transpose(T.TR[:, :], T.WT[:, :]), 0.1)
-        for a in range(4):
-            for h in range(2):
-                for k in range(2):
-                    dma("s", "dw%d" % t, T[DD][2 * a + h:2 * a + h + 1, 384 * k:384 * k + 384],
-                        T.TR[32 * a:32 * a + 24, 32 * k + 16 * h:32 * k + 16 * h + 16], [V("TR")], [V(DD)])
-        for q in range(16):
-            dma("s", "dr%d" % t, T[TT][q::16, :], T[DD][:], [V(DD)], [V(TT)])
+        for k in range(2):
+            D, r, w = "D%s%d" % ("MP"[k], t), V("TR", 32 * k, 32 * k + 32), V("WT", 32 * k, 32 * k + 32)
+            turn32(r, w)
+            for a in range(4):
+                for h in range(2):
+                    dma("s", "%s%d" % (("dw", "ew")[k], t), T[D][2 * a + h:2 * a + h + 1, :],
+                        T.TR[32 * a:32 * a + 24, 32 * k + 16 * h:32 * k + 16 * h + 16], [r], [V(D)])
+            for q in range(16):
+                dma("s", "%s%d" % (("dr", "er")[k], t), T[TT][q::16, 384 * k:384 * k + 384], T[D][:], [V(D)], [V(TT, 384 * k, 384 * k + 384)])
         if t < 2:
             S2, k = "S%d" % (t + 1), "sh%d" % t
             rs, ws = [V(SN)], [V(S2)]
@@ -525,14 +536,14 @@ def rank_program(g, core, T, topo):
                 dma("s", k, T[S2][0::16, 0:4], T[SN][15::16, 92:96], rs, ws)
         tt(V("GI"), V("TB"), V("MASK", 0, 384), A.mult, V("IL"))
         scan("SCI", "GI", 384)
-        tt(V("TD"), V("SCI", 15, 384, 16), V("IDS"), A.mult)
+        tt(V("TD"), V("SCI", 15, 384, 16), V("PS"), A.not_equal)
         ts(V("TE"), V("TD"), 96.0, A.mult)
         tt(V("POSB"), V("POSB"), V("TE"), A.add)
         if t < 2:
-            tt(V("PP"), V("PP"), V("TD"), A.add)
+            tt(V("PP"), V("PL"), V("TD"), A.add)
         if t == 1:
             ts(V("TD"), V("PP"), 192.0, A.is_equal, 192.0, A.mult)
-            ts(V("TE"), V("PP"), 0.0, A.is_equal, -256.0, A.mult)
+            ts(V("TE"), V("PP"), 512.0, A.is_equal, -256.0, A.mult)
             tt(V("POSB"), V("POSB"), V("TD"), A.add)
             tt(V("POSB"), V("POSB"), V("TE"), A.add)
         cp(V("POS"), V("POSB"))
@@ -541,30 +552,37 @@ def rank_program(g, core, T, topo):
         for b in range(4):
             act(V("VH", 384 * b, 384 * b + 192), V("P%d" % b, 0, 192), 0.5)
         for b in range(4):
-            v = V("AH", 384 * b, 384 * b + 384)
-            tt(V("ZT", b, 1536, 4), V("VH", 384 * b, 384 * b + 384), v, A.add, V("POS"))
-            act(V("AF", 384 * b, 384 * b + 384), v, 2.0)
-        quant("qz", 384, V("ZT"))
-        for b in range(4):
-            mm("P%d" % b, 384, "qw", 128 * b, "qz")
-            act(V("GB", 384 * b, 384 * b + 384), V("P%d" % b, 0, 384), 0.0078125)
+            act(V("AF", 384 * b, 384 * b + 384), V("AH", 384 * b, 384 * b + 384), 2.0)
+        for h in range(2):
+            for b in range(4):
+                c = 384 * b + 192 * h
+                tt(V("ZT", 768 * h + b, 768 * h + 768, 4), V("VH", 384 * b, 384 * b + 384), V("AH", c, c + 192), A.add, V("POS", 12 * h, 12 * h + 12))
+            quant("qz", 192, V("ZT", 768 * h, 768 * h + 768), 192 * h)
+            for b in range(4):
+                c = 384 * b + 192 * h
+                mm("P%d" % (b + 4 * h), 192, "qw", 128 * b, "qz", 192 * h)
+                act(V("GB", c, c + 192), V("P%d" % (b + 4 * h), 0, 192), 0.0078125)
         w = wrapped(V(TT, 0, 384), V("POS"))
         cp(V("ML"), w)
         if t < 2:
             prep1(t + 1)
-        for b in range(4):
-            tt(V("XT", b, 1536, 4), V("GB", 384 * b, 384 * b + 384), V("AF", 384 * b, 384 * b + 384), A.add, V("ML"))
+        for h in range(2):
+            for b in range(4):
+                c = 384 * b + 192 * h
+                tt(V("XT", 768 * h + b, 768 * h + 768, 4), V("GB", 384 * b, 384 * b + 384), V("AF", c, c + 192), A.add, V("ML", 12 * h, 12 * h + 12))
 
     quant("qv", 128, V("VV"))
-    quant("qx", 384, V("XT"))
-    mm("PSC", 384, "qv", 0, "qx")
+    for h in range(2):
+        c, e = 192 * h, 192 * h + 192
+        quant("qx", 192, V("XT", 4 * c, 4 * e), c)
+        mm("P%d" % (4 + h), 192, "qv", 0, "qx", c)
+        act(V("YS", c, e), V("P%d" % (4 + h), 0, 192))
+        dma("a", "y", T.y[:, c:e], T.YS[:, c:e], [V("YS", c, e)], [])
+        dma("s", "out", T.oc[:, 4 * c:4 * e], T.qx[:, c:e].bitcast(dt.uint8), [V("qx", c, e)], [])
+        for k in range(4):
+            dma("s", "out", T.osc[4 * k:4 * k + 4, c:e], T.sqx[32 * k:32 * k + 4, c:e], [V("sqx", c, e)], [])
     act(V("OMB", 0, 384, 2), V("TT2", 384, 576))
     act(V("OMB", 1, 384, 2), V("TT2", 576, 768))
     act(V("OMB", 384, 768), V("TT2", 0, 384), 1.0, V("POS"))
     dma("s", "om", T.om[:], T.OMB[0::16, :], [V("OMB")], [])
-    act(V("YS"), V("PSC", 0, 384))
-    dma("a", "y", T.y[:], T.YS[:], [V("YS")], [])
-    dma("s", "out", T.oc[:], T.qx[:].bitcast(dt.uint8), [V("qx")], [])
-    for k in range(4):
-        dma("s", "out", T.osc[4 * k:4 * k + 4, :], T.sqx[32 * k:32 * k + 4, :], [V("sqx")], [])
     emit_all()

import numpy as np
from concourse.mybir import dt, AluOpType, ActivationFunctionType

A = AluOpType
COPY = ActivationFunctionType.Copy
STEP = (1, 2, 3)
F8 = "float8_e4m3fn_x4"
ORDER = {}
TRIES = 1600

SCRATCH = {}


def _sb(name, n, d="float32", where="sbuf"):
    SCRATCH[name] = (where, [128, n], d)


for _n, _w in (("X0", 1536), ("UU", 512), ("VV", 512), ("XT", 1536), ("ZT", 1536), ("ET", 768), ("CE", 2048), ("FH", 1536),
               ("VH", 1536), ("AH", 1536), ("AF", 1536), ("MASK", 576), ("RST", 576), ("TB", 256), ("N16", 576)):
    _sb(_n, _w, "bfloat16")
for _n, _w in (("qx", 384), ("qz", 384), ("qe", 192), ("qu", 128), ("qv", 128), ("qur", 128), ("qw", 512), ("qce", 512),
               ("le0", 192), ("le1", 192), ("le2", 192)):
    _sb(_n, _w, F8)
    _sb("s" + _n, _w, "uint8")
for _n, _w in (("SS", 384), ("SGR", 192), ("GB", 1536), ("YS", 384), ("WT", 64), ("TR", 64), ("TT0", 768), ("TT1", 768), ("TT2", 768),
               ("OMB", 768), ("PR", 384), ("IOT", 384), ("MN", 384), ("IW", 384), ("OCR", 384), ("ABI", 128), ("RI", 384), ("TI", 384), ("IDN", 128),
               ("DEL", 96), ("TMP", 96), ("QQ", 96)):
    _sb(_n, _w)
for _n, _w in (("OW", 24), ("MW", 24), ("OR", 384), ("MR", 384), ("S0", 96), ("S1", 96), ("S2", 96), ("SN0", 96), ("SN1", 96), ("SN2", 96)):
    _sb(_n, _w, "int32")
PART, TOP = {}, {}


def _parts(buf, d, more, items):
    at = 0
    for n, w in items:
        PART[n] = (buf, at, w)
        at += -(-w // 16) * 16
    TOP[buf] = at
    _sb(buf, at + more, d)


_parts("GMB", "float32", 8064, (("GM", 384), ("SC", 384)))
_parts("GFB", "bfloat16", 5760, (("GF", 576), ("SCF", 576), ("GI", 384), ("SCI", 384)))
_parts("FS", "float32", 4096, (
    ("DSG", 24), ("NN", 12), ("XX", 48), ("DQ", 48), ("XD", 48), ("NM", 24), ("D0", 24), ("DIS", 12), ("DO", 12), ("KID", 12), ("WM", 12),
    ("K0", 24), ("K1", 24), ("KC0", 24), ("KC1", 24), ("PQF", 1), ("PQ2", 1), ("P24", 1), ("M15", 1), ("T24", 24), ("NX", 24), ("PL", 24),
    ("POSB", 24), ("TD", 24), ("TE", 24), ("SW", 4), ("RW0", 24), ("ITA", 24)))
_parts("IS", "int32", 4096, (
    ("KM", 24), ("SM", 24), ("KP", 24), ("TPI", 24), ("DK", 12), ("FK", 12), ("KA", 24), ("KMK", 24), ("WI", 24), ("NB", 24),
    ("KN", 24), ("DM", 24), ("FM", 24), ("PP", 24), ("PK", 24), ("PS", 24), ("PQI", 1), ("PQ0", 1), ("CKI", 24), ("CKJ", 24)))
_parts("US", "uint16", 2048, (
    ("OL", 24), ("CK", 24), ("N24", 24), ("UL", 8), ("FLL", 36), ("LL", 12), ("RL", 12), ("TPL", 24), ("LM", 24),
    ("POS", 24), ("ML", 24), ("IL", 24), ("MS", 24), ("OS", 24)))
for _n in ("P0", "P1", "P2", "P3", "P4", "P5", "P6", "P7"):
    _sb(_n, 512, "float32", "psum")
for _n in ("DM0", "DM1", "DM2", "DP0", "DP1", "DP2"):
    SCRATCH[_n] = ("dram", [8, 384], "float32")
SEMAPHORES = ["cv", "ca", "ct", "cp", "re0", "re1", "re2", "ls"] + ["d%d" % k for k in range(60)]


def rank_program(g, core, T, topo):
    rank = T.rank_of(core)
    if rank is None:
        return
    ENG = {"v": g.vector, "a": g.scalar, "t": g.tensor, "p": g, "s": g.sync}

    now = dict(PART)
    top = dict(TOP)

    def V(name, lo=0, hi=None, step=1):
        buf, at, w = now[name] if name in now else (name, 0, SCRATCH[name][1][1])
        hi = w if hi is None else hi
        return (buf, at + lo, at + hi, step, name if name in now and (lo, hi, step) == (0, w, 1) else None)

    def fresh(v):
        if v[4] is None:
            return v
        buf, at, w = now[v[4]]
        now[v[4]] = (buf, top[buf], w)
        top[buf] += -(-w // 16) * 16
        assert top[buf] <= SCRATCH[buf][1][1]
        return V(v[4])

    def ap(v):
        return T[v[0]][:, v[1]:v[2]:v[3]] if v[3] > 1 else T[v[0]][:, v[1]:v[2]]

    def by(v):
        return ap(v).bitcast(dt.uint8)

    def ind(v, l):
        return ap(v).indirect(ap(l)) if l else ap(v)

    def width(v):
        return -(-(v[2] - v[1]) // v[3])

    def meet(a, b):
        if SCRATCH[a[0]][0] == "psum":
            return True
        if a[2] <= b[1] or b[2] <= a[1]:
            return False
        return not (a[3] == b[3] > 1 and (a[1] - b[1]) % a[3])

    ops, hist = [], {}

    def add(q, rd, wr, emit, cost, lat=0.0, src=None, n=0):
        i = len(ops)
        src = src or q
        pred = set()
        for w, vs in ((False, rd), (True, wr)):
            for v in vs:
                for e in hist.get(v[0], ()):
                    if (w or e[0]) and meet(v, e[1]) and not (src[0] == "d" and ops[e[2]]["src"][:3] == src[:3]):
                        pred.add(e[2])
        ops.append({"q": q, "pred": sorted(pred), "emit": emit, "cost": cost, "lat": lat, "src": src, "n": n})
        for v in wr:
            hist[v[0]] = [e for e in hist.get(v[0], []) if src[0] == "d" or not (v[3] == 1 and v[1] <= e[1][1] and e[1][2] <= v[2])]
            hist[v[0]].append((True, v, i))
        for v in rd:
            hist.setdefault(v[0], []).append((False, v, i))
        return i

    CY = 0.00095

    def dve(n, lst, rate=1.0):
        return 0.05 + 1.5 * CY * n if lst else 0.02 + max(64, rate * n) * CY

    def sb(*vs):
        return 2.0 if all(SCRATCH[v[0]][0] == "sbuf" for v in vs) else 1.0

    def dma(q, key, out, in_, rd, wr):
        add(q, rd, wr, lambda e: e.dma_start(out, in_), 0.08, 2.4, "d" + key)

    def tt(out, a, b, f, lst=None):
        out = fresh(out)
        add("v", [a, b] + ([lst] if lst else []), [out],
            lambda e: e.tensor_tensor(ap(out), ind(a, lst), ap(b), f), dve(width(out), lst, sb(a, b)))

    def ts(out, a, s1, f1, s2=None, f2=None, lst=None, col=None):
        out = fresh(out)
        i = [a] + ([lst] if lst else []) + ([col] if col else [])
        if f2 is None:
            add("v", i, [out], lambda e: e.tensor_scalar(ap(out), ind(a, lst), ap(col) if col else s1, None, f1), dve(width(out), lst))
        else:
            add("v", i, [out], lambda e: e.tensor_scalar(ap(out), ind(a, lst), s1, s2, f1, f2), dve(width(out), lst))

    def cp(out, a, lst=None):
        out = fresh(out)
        add("v", [a] + ([lst] if lst else []), [out], lambda e: e.tensor_copy(ap(out), ind(a, lst)), dve(width(out), lst))

    def act(out, a, scale=1.0, lst=None, func=COPY, bias=0.0):
        add("a", [a] + ([lst] if lst else []), [out],
            lambda e: e.activation(ap(out), ind(a, lst), func, **({} if (scale, bias) == (1.0, 0.0) else {"scale": scale, "bias": bias})), dve(width(out), lst) + 0.02)

    def fill(v, c):
        add("v", [], [v], lambda e: e.memset(ap(v), c), dve(width(v), None, 0.5))

    def iota(v, pattern, base, ch):
        add("p", [], [v], lambda e: e.iota(ap(v), pattern, base, ch, allow_small_or_imprecise_dtypes=True), 0.13 + 2 * CY * width(v))

    def quant(q, n, src, lo=0):
        c, s = V(q, lo, lo + n), V("s" + q, lo, lo + n)
        add("v", [src], [c, s], lambda e: e.quantize_mx(ap(c), ap(s), ap(src)), 0.03 + 0.0010 * n)

    def mm(bank, n, l, llo, r, lo=0):
        o, a, b = V(bank, 0, n), V(l, llo, llo + 128), V(r, lo, lo + n)
        c, d = V("s" + l, llo, llo + 128), V("s" + r, lo, lo + n)
        add("t", [a, b, c, d], [o], lambda e: e.matmul_mx(ap(o), ap(a), ap(c), ap(b), ap(d), True, True), (n + 16) * 0.0007)

    def scan(out, a, n):
        x, m = V(a, 0, n), V("RST", 0, n)
        o = fresh(V(out, 0, n))
        add("v", [x, m], [o], lambda e: e.tensor_tensor_scan(ap(o), ap(m), ap(x), 0.0, A.mult, A.add), dve(n, None, 1.0 if out == "SC" else 0.5))

    def turn32(out, in_):
        add("v", [in_], [out], lambda e: e.transpose(ap(out), ap(in_)), 0.1)

    def send(t, dst):
        eng = topo.engines(core, dst)[::2]
        mask = sum(1 << e for e in eng)
        rid, pid = topo.addr(dst)[:2]
        c, s, lc, ls, sem = V("qe"), V("sqe"), V("le%d" % t), V("sle%d" % t), "re%d" % t

        def emit(e):
            e.remote_dma(by(lc), by(c), T.sem[sem], T.sem.ls, pid, rid, mask)
            e.remote_dma(ap(ls), ap(s), T.sem[sem], T.sem.ls, pid, rid, mask)
        i = add("p", [c, s], [], emit, 0.3, 1.0, "ls", 2 * len(eng))
        j = add("far", [], [lc, ls], None, 0.0, 3.0, sem, 2 * len(eng))
        ops[j]["pred"].append(i)

    WAKE = 0.17

    def plan(noise, patience):
        n = len(ops)
        succ, left = [[] for o in ops], [len(o["pred"]) for o in ops]
        for i, o in enumerate(ops):
            for p in o["pred"]:
                succ[p].append(i)
        prio = [0.0] * n
        for i in range(n - 1, -1, -1):
            prio[i] = ops[i]["cost"] + ops[i]["lat"] + max([prio[j] + WAKE for j in succ[i]] or [0.0])
        if noise is not None:
            prio = [p + x for p, x in zip(prio, noise)]
        free, est, order, end, ready = {}, [0.0] * n, [], 0.0, {}
        for i in range(n):
            if not left[i]:
                ready.setdefault(ops[i]["q"], []).append(i)
        while True:
            best = None
            for q, r in ready.items():
                if not r:
                    continue
                f = free.get(q, 0.0)
                s = max(f, min(est[i] for i in r))
                c = max((i for i in r if est[i] <= s), key=lambda i: (prio[i], -i))
                for i in r:
                    if prio[i] > prio[c] + 1.0 and est[i] < s + patience * ops[c]["cost"]:
                        c = i
                s = max(f, est[c])
                if best is None or s < best[0]:
                    best = (s, c, q)
            if best is None:
                return end, order
            s, c, q = best
            ready[q].remove(c)
            order.append(c)
            free[q] = s + ops[c]["cost"]
            done = free[q] + ops[c]["lat"]
            end = max(end, done)
            for j in succ[c]:
                est[j] = max(est[j], done + WAKE)
                left[j] -= 1
                if not left[j]:
                    ready.setdefault(ops[j]["q"], []).append(j)

    def emit_all():
        if "order" not in ORDER:
            rng = np.random.default_rng(7)
            best, noise, patience = None, None, 0.3
            for slope in (0.0, 0.001, 0.002, 0.004):
                for p in (0.0, 0.3, 0.7):
                    v = [-slope * i for i in range(len(ops))]
                    x = plan(v, p)
                    if best is None or x[0] < best[0]:
                        best, noise, patience = x, v, p
            for k in range(TRIES):
                f = rng.random(len(ops)) < (0.02, 0.1, 0.4)[k % 3]
                v = [a + float(b) for a, b in zip(noise, f * rng.normal(0.0, (1.0, 0.5, 0.3)[k % 3], len(ops)))]
                x = plan(v, patience)
                if x[0] <= best[0]:
                    best, noise = x, v
            ORDER["order"], ORDER["end"] = best[1], best[0]
        known = {q: {} for q in ENG}
        tot, keys, mark = {}, {}, {}
        for i in ORDER["order"]:
            o = ops[i]
            src, q = o["src"], o["q"]
            if q not in ENG:
                keys[src] = T.sem[src]
                tot[src] = o["n"]
                mark[i] = (tot[src], {})
                continue
            need = {}
            for p in o["pred"]:
                s = ops[p]["src"]
                c, clk = (tot[s] if s[0] == "d" else mark[p][0]), mark[p][1]
                if s not in need or need[s][0] < c:
                    need[s] = (c, clk)
            for s in sorted(need, key=lambda s: (s == q, -len(need[s][1]), s)):
                if known[q].get(s, 0) < need[s][0]:
                    ENG[q].wait_ge(keys[s], need[s][0])
                    known[q][s] = need[s][0]
                    for y, x in need[s][1].items():
                        known[q][y] = max(known[q].get(y, 0), x)
            ins = o["emit"](ENG[q])
            if src == q:
                keys[src] = T.sem["c" + q]
                tot[src] = tot.get(src, 0) + 1
                ins.then_inc(keys[src], 1)
            elif src[0] == "d":
                if src not in keys:
                    keys[src] = T.sem["d%d" % len(keys)]
                tot[src] = tot.get(src, 0) + 16
                ins.then_inc(keys[src], 16)
            else:
                keys[src] = T.sem[src]
                tot[src] = tot.get(src, 0) + o["n"]
            mark[i] = (tot[src], dict(known[q]))
        for s, c in tot.items():
            if known["p"].get(s, 0) < c:
                g.wait_ge(keys[s], c)

    def wrapped(src, lst):
        tt(V("GM"), src, V("MASK", 0, 384), A.mult, lst)
        scan("SC", "GM", 384)
        return V("SC", 15, 384, 16)

    def fld(s, f, side=None):
        return V(s, f, 96, 4) if side is None else V(s, 48 * side + f, 48 * side + 48, 4)

    def prep1(t):
        S = "S%d" % t
        key = fld(S, 3)
        if t == 1:
            ts(V("KP"), key, -1, A.add)
            key = V("KP")
        ts(V("KM"), key, 511, A.bitwise_and, 1, A.logical_shift_right)
        ts(V("SM"), key, 1, A.bitwise_and)
        tt(V("DIS"), V("KM", 0, 12), V("KID"), A.is_equal)
        if t == 1:
            tt(V("DIS"), V("DIS"), V("WM"), A.max)
        tt(V("DO"), fld(S, 2, 0), fld(S, 2, 1), A.subtract)
        cp(V("LL"), fld(S, 2, 0))
        tt(V("DO"), V("DIS"), V("DO"), A.mult)
        tt(V("DO"), V("DO"), fld(S, 2, 1), A.add)
        cp(V("RL"), V("DO"))
        cp(V("FLL", 0, 24), V("KM"))
        tt(V("DK"), fld(S, 3, 0), fld(S, 3, 1), A.subtract)
        ts(V("FK"), V("DK"), 9, A.arith_shift_right)
        ts(V("NN"), V("FK"), 0.0, A.not_equal)
        ts(V("DSG"), V("SM"), -2.0, A.mult, 1.0, A.add)
        ts(V("KA"), fld(S, 3), 3072, A.bitwise_and)
        tt(V("KMK"), V("KC1" if t == 1 else "KC0"), V("KA"), A.subtract)
        if t == 0:
            ts(V("TPI"), V("SM"), -192, A.mult, 192, A.add)
        else:
            ts(V("TPI"), V("SM"), 191, A.mult, 1 if t == 1 else 0, A.add)
        tt(V("TPI"), V("TPI"), V("KM"), A.add)
        if t == 2:
            ts(V("NB"), fld(S, 3), 511, A.bitwise_and)
            ts(V("NB"), V("NB"), 1, A.is_equal, 192, A.mult)
            tt(V("TPI"), V("TPI"), V("NB"), A.add)
        ts(V("TPL"), V("TPI"), 383, A.min)

    def prep2(t):
        S = "S%d" % t
        w = wrapped(V("OCR") if t == 0 else V("TT%d" % (t - 1), 384, 768), V("TPL"))
        cp(V("WI"), w)
        ts(V("KN"), V("WI"), 9, A.logical_shift_right)
        ts(V("NB"), V("WI"), 511, A.bitwise_and)
        if t == 0:
            ts(V("TPI"), fld(S, 1), 511, A.bitwise_and)
            tt(V("D0"), V("TPI"), V("DSG"), A.add)
            ts(V("TE"), V("NB"), 191.5, A.is_gt, 2048.0, A.mult)
            tt(V("D0"), V("KN"), V("D0"), A.is_gt)
            tt(V("TE"), V("TE"), V("KN"), A.add)
            ts(V("D0"), V("D0"), 1024.0, A.mult)
            tt(V("KN"), V("TE"), V("D0"), A.add)
        tt(V("DM"), V("KMK"), V("KN"), A.subtract)
        tt(V("DM"), V("DM"), V("DSG"), A.mult)
        ts(V("FM"), V("DM"), 9, A.arith_shift_right)
        ts(V("NM"), V("FM"), 0.0, A.is_equal)
        ts(V("NX"), V("FM"), 0.0, A.not_equal)
        tt(V("D0"), V("NB"), fld(S, 0), A.subtract)
        tt(fld("DEL", 0), V("NM"), V("D0"), A.mult)
        tt(fld("DEL", 1), V("NX"), V("DSG"), A.mult)

    def items(t):
        src = V("PP")
        if t == 1:
            ts(V("PK"), V("PP"), -1, A.add)
            src = V("PK")
        ts(V("PS"), src, 1, A.bitwise_and)
        ts(V("PK"), src, 511, A.bitwise_and, 1, A.logical_shift_right)
        cp(V("IL"), V("PK"))
        ts(V("PL"), V("PK"), 2, A.mult, t % 2, A.add)
        ts(V("TD"), V("PK"), 96.0, A.is_ge, 96.0, A.mult)
        tt(V("POSB"), V("PK"), V("TD"), A.add)

    dma("s", "ow", T.OW[:], T.o[:], [], [V("OW")])
    for q in range(16):
        dma("sa"[q % 2], "or" + "sa"[q % 2], T.OR[q::16, :], T.o[:], [], [V("OR")])
    for q in range(16):
        dma("sa"[q % 2], "mr" + "sa"[q % 2], T.MR[q::16, :], T.m[:], [], [V("MR")])
    dma("s", "mw", T.MW[:], T.m[:], [], [V("MW")])
    dma("a", "x", T.X0[:], T.x[:], [], [V("X0")])
    dma("a", "u", T.UU[:], T.u[:], [], [V("UU")])
    dma("s", "wc", T.qw[:].bitcast(dt.uint8), T.wc[:], [], [V("qw")])
    dma("s", "ws", T.sqw[:], T.ws[:], [], [V("sqw")])
    dma("s", "v", T.VV[:], T.v[:], [], [V("VV")])

    iota(V("PQI"), [[1, 1]], 0, 1)
    iota(V("K0"), [[1, 2], [32, 12]], 0, 0)
    iota(V("IOT"), [[1, 384]], 0, 0)
    iota(V("N16"), [[0, 36], [1, 16]], 0, 0)
    iota(V("ITA"), [[1, 24]], 0, 0)
    iota(V("IDN"), [[1, 128]], 0, -1)
    iota(V("T24"), [[16, 24]], 0, 0)
    fill(V("TB", 192, 256), 0.0)
    for n in ("WT", "TMP", "XX", "DEL"):
        fill(V(n), 0.0)
    ts(V("PQ0"), V("PQI"), 15, A.bitwise_and)
    cp(V("PQF"), V("PQ0"))
    ts(V("PQ2"), V("PQF"), 2.0, A.mult)
    ts(V("P24"), V("PQF"), 24.0, A.mult)
    ts(V("M15"), V("PQF"), 15.0, A.is_equal)
    ts(V("K0"), V("K0"), None, A.add, col=V("PQ2"))
    ts(V("N24"), V("ITA"), None, A.add, col=V("P24"))
    cp(V("CKI"), V("K0"))
    ts(V("CKJ"), V("CKI"), 15, A.bitwise_and)
    ts(V("CKJ"), V("CKJ"), 24, A.mult)
    ts(V("CKI"), V("CKI"), 4, A.logical_shift_right)
    tt(V("CKI"), V("CKI"), V("CKJ"), A.add)
    cp(V("CK"), V("CKI"))
    ts(V("MASK"), V("N16"), None, A.is_equal, col=V("PQF"))
    act(V("RST"), V("N16"), func=ActivationFunctionType.Sign)
    ts(V("KID"), V("T24", 0, 12), None, A.add, col=V("PQF"))
    cp(V("FLL", 24, 36), V("KID"))
    ts(V("KC0"), V("K0"), 3072.0, A.add)
    ts(V("TD"), V("K0"), 1.0, A.add)
    ts(V("DO"), V("TD", 12, 24), 384.0, A.is_equal, -384.0, A.mult)
    cp(V("K1", 0, 12), V("TD", 0, 12))
    tt(V("K1", 12, 24), V("TD", 12, 24), V("DO"), A.add)
    ts(V("KC1"), V("K1"), 3072.0, A.add)
    ts(V("WM"), V("K1", 0, 12), 383.0, A.is_equal)
    act(V("ABI"), V("IDN"), func=ActivationFunctionType.Abs)
    for b in range(4):
        act(V("CE", 512 * b, 512 * b + 512), V("N16", 0, 512), 0.0)
        act(V("CE", 512 * b + b, 512 * b + 512, 4), V("ABI"), -1.0, func=ActivationFunctionType.Relu, bias=1.0)
    quant("qce", 512, V("CE"))

    quant("qu", 128, V("UU"))
    cp(V("UL"), V("T24", 0, 8))
    ul = V("UL")
    add("v", [V("qu"), ul], [V("qur")], lambda e: e.tensor_copy(T.qur[:, 0:128].bitcast(dt.uint32), T.qu[:, 0:128].bitcast(dt.uint32).indirect(ap(ul))), 0.25)
    act(V("squr"), V("squ"), lst=ul)

    cp(V("OL"), V("OW"))
    ol = V("OL")
    add("v", [ol, V("IOT")], [V("PR")], lambda e: e.tensor_copy(ind(V("PR"), ol), ap(V("IOT"))), 1.2)
    cp(V("ML"), V("MW"))
    act(V("RI"), V("PR"), 512.0, V("ML"))
    cp(V("MN"), V("MR"), V("N24"))
    tt(V("TI"), V("RI"), V("MN"), A.add)
    w = wrapped(V("OR"), V("CK"))
    cp(V("OS"), w)
    cp(fld("S0", 2), w)
    tt(V("IW"), V("RI"), V("IOT"), A.add)
    act(V("OCR"), V("IW"), 1.0, V("OS"))
    w = wrapped(V("TI"), V("OS"))
    cp(V("WI"), w)
    ts(V("PS"), V("WI"), 9, A.logical_shift_right)
    ts(fld("S0", 0), V("WI"), 511, A.bitwise_and)
    tt(V("TD"), V("PS"), V("K0"), A.is_gt)
    ts(V("TE"), fld("S0", 2), 191.5, A.is_gt, 2048.0, A.mult)
    ts(V("TD"), V("TD"), 1024.0, A.mult)
    tt(fld("S0", 1), V("TD"), V("PS"), A.add)
    tt(fld("S0", 3), fld("S0", 1), V("TE"), A.add)
    tt(V("GM"), V("PR"), V("MASK", 0, 384), A.mult)
    scan("SC", "GM", 384)
    cp(V("PP"), V("SC", 15, 384, 16))
    prep1(0)

    for t in range(3):
        S, SN, TT, le = "S%d" % t, "SN%d" % t, "TT%d" % t, "le%d" % t
        for h in range(2):
            quant("qx", 192, V("XT" if t else "X0", 768 * h, 768 * h + 768), 192 * h)
            mm("P%d" % (4 + h), 192, "qur", 0, "qx", 192 * h)
            act(V("SS", 192 * h, 192 * h + 192), V("P%d" % (4 + h), 0, 192))
        for b in range(4):
            mm("P%d" % b, 384, "qce", 128 * b, "qx")
        act(V("SGR"), V("SS"), 1.0, V("RL"))
        for b in range(4):
            act(V("FH", 384 * b, 384 * b + 384), V("P%d" % b, 0, 384), 0.5)
        for b in range(4):
            act(V("AH", 384 * b, 384 * b + 384), V("FH", 384 * b, 384 * b + 384), 1.0, V("ML"))
        prep2(t)
        items(t)
        tt(V("TB", 0, 192), V("SS"), V("SGR"), A.is_gt, V("LL"))
        tt(V("GF"), V("TB"), V("MASK"), A.mult, V("FLL"))
        scan("SCF", "GF", 576)
        fm, tf = V("SCF", 15, 384, 16), V("SCF", 399, 576, 16)
        tt(fld("TMP", 0), fm, fld("DEL", 0), A.mult)
        tt(fld("TMP", 1), fm, fld("DEL", 1), A.mult)
        tt(V("XX", 0, 48, 4), tf, V("NN"), A.mult)
        tt(V("XX", 1, 48, 4), tf, V("NN"), A.mult)
        cp(V("XX", 2, 48, 4), tf)
        tt(V("QQ"), V("TMP"), V(S), A.add)
        tt(V("DQ"), V("QQ", 48, 96), V("QQ", 0, 48), A.subtract)
        tt(V("XD"), V("DQ"), V("XX"), A.mult)
        tt(V(SN, 0, 48), V("QQ", 0, 48), V("XD"), A.add)
        tt(V(SN, 48, 96), V("QQ", 48, 96), V("XD"), A.subtract)
        cp(V("LM", 0, 6), V(SN, 0, 24, 4))
        if t == 1:
            tt(V("SW", 0, 1), V(SN, 92, 93), V(SN, 68, 69), A.subtract)
            ts(V("SW", 1, 2), V("SW", 0, 1), None, A.mult, col=V("M15"))
            tt(V("SW", 2, 3), V(SN, 68, 69), V("SW", 1, 2), A.add)
            tt(V("SW", 3, 4), V(SN, 92, 93), V("SW", 1, 2), A.subtract)
            cp(V("LM", 6, 11), V(SN, 48, 68, 4))
            cp(V("LM", 11, 12), V("SW", 2, 3))
            cp(V("LM", 18, 23), V(SN, 72, 92, 4))
            cp(V("LM", 23, 24), V("SW", 3, 4))
        else:
            cp(V("LM", 6, 12), V(SN, 48, 72, 4))
            cp(V("LM", 18, 24), V(SN, 72, 96, 4))
        cp(V("LM", 12, 18), V(SN, 24, 48, 4))
        for b in (0, 1):
            ts(V("ET", b, 768, 4), V("FH", 384 * b, 384 * b + 384), 2.0, A.mult, lst=V("LM", 0, 12))
        for b in (2, 3):
            act(V("ET", b, 768, 4), V("FH", 384 * b, 384 * b + 384), 2.0, V("LM", 0, 12))
        quant("qe", 192, V("ET"))
        send(t, T.cores[rank ^ STEP[t]])
        for b in range(4):
            act(V("VH", 384 * b + 192, 384 * b + 384), V("FH", 384 * b, 384 * b + 384), 1.0, V("LM", 12, 24))
        cp(V("WT", 0, 24), V("LM"))
        if t < 2:
            ts(V("TE"), fld(SN, 2), 191.5, A.is_gt, 2048.0, A.mult)
            tt(fld(SN, 3), fld(SN, 1), V("TE"), A.add)
            ts(V("TD"), fld(SN, 3), 512.0, A.mult)
            tt(V("WT", 32, 56), V("TD"), fld(SN, 2), A.add)
        else:
            cp(V("WT", 32, 56), fld(SN, 2))
        for k in range(2):
            D, r, w = "D%s%d" % ("MP"[k], t), V("TR", 32 * k, 32 * k + 32), V("WT", 32 * k, 32 * k + 32)
            turn32(r, w)
            for a in range(4):
                for h in range(2):
                    dma("s", "%s%d" % (("dw", "ew")[k], t), T[D][2 * a + h:2 * a + h + 1, :],
                        T.TR[32 * a:32 * a + 24, 32 * k + 16 * h:32 * k + 16 * h + 16], [r], [V(D)])
            for q in range(16):
                dma("s", "%s%d" % (("dr", "er")[k], t), T[TT][q::16, 384 * k:384 * k + 384], T[D][:], [V(D)], [V(TT, 384 * k, 384 * k + 384)])
        if t < 2:
            S2, k = "S%d" % (t + 1), "sh%d" % t
            rs, ws = [V(SN)], [V(S2)]
            if t == 0:
                dma("s", k, T[S2][:, 0:48], T[SN][:, 48:96], rs, ws)
                for i in range(8):
                    dma("s", k, T[S2][16 * i:16 * i + 15, 48:96], T[SN][16 * i + 1:16 * i + 16, 0:48], rs, ws)
                dma("s", k, T[S2][15::16, 48:92], T[SN][0::16, 4:48], rs, ws)
                dma("s", k, T[S2][15::16, 92:96], T[SN][0::16, 0:4], rs, ws)
            else:
                dma("s", k, T[S2][:, 48:96], T[SN][:, 0:48], rs, ws)
                for i in range(8):
                    dma("s", k, T[S2][16 * i + 1:16 * i + 16, 0:48], T[SN][16 * i:16 * i + 15, 48:96], rs, ws)
                dma("s", k, T[S2][0::16, 4:48], T[SN][15::16, 48:92], rs, ws)
                dma("s", k, T[S2][0::16, 0:4], T[SN][15::16, 92:96], rs, ws)
        tt(V("GI"), V("TB"), V("MASK", 0, 384), A.mult, V("IL"))
        scan("SCI", "GI", 384)
        tt(V("TD"), V("SCI", 15, 384, 16), V("PS"), A.not_equal)
        ts(V("TE"), V("TD"), 96.0, A.mult)
        tt(V("POSB"), V("POSB"), V("TE"), A.add)
        if t < 2:
            tt(V("PP"), V("PL"), V("TD"), A.add)
        if t == 1:
            ts(V("TD"), V("PP"), 192.0, A.is_equal, 192.0, A.mult)
            ts(V("TE"), V("PP"), 512.0, A.is_equal, -256.0, A.mult)
            tt(V("POSB"), V("POSB"), V("TD"), A.add)
            tt(V("POSB"), V("POSB"), V("TE"), A.add)
        cp(V("POS"), V("POSB"))
        for b in range(4):
            mm("P%d" % b, 192, "qce", 128 * b, le)
        for b in range(4):
            act(V("VH", 384 * b, 384 * b + 192), V("P%d" % b, 0, 192), 0.5)
        for b in range(4):
            act(V("AF", 384 * b, 384 * b + 384), V("AH", 384 * b, 384 * b + 384), 2.0)
        for h in range(2):
            for b in range(4):
                c = 384 * b + 192 * h
                tt(V("ZT", 768 * h + b, 768 * h + 768, 4), V("VH", 384 * b, 384 * b + 384), V("AH", c, c + 192), A.add, V("POS", 12 * h, 12 * h + 12))
            quant("qz", 192, V("ZT", 768 * h, 768 * h + 768), 192 * h)
            for b in range(4):
                c = 384 * b + 192 * h
                mm("P%d" % (b + 4 * h), 192, "qw", 128 * b, "qz", 192 * h)
                act(V("GB", c, c + 192), V("P%d" % (b + 4 * h), 0, 192), 0.0078125)
        w = wrapped(V(TT, 0, 384), V("POS"))
        cp(V("ML"), w)
        if t < 2:
            prep1(t + 1)
        for h in range(2):
            for b in range(4):
                c = 384 * b + 192 * h
                tt(V("XT", 768 * h + b, 768 * h + 768, 4), V("GB", 384 * b, 384 * b + 384), V("AF", c, c + 192), A.add, V("ML", 12 * h, 12 * h + 12))

    quant("qv", 128, V("VV"))
    for h in range(2):
        c, e = 192 * h, 192 * h + 192
        quant("qx", 192, V("XT", 4 * c, 4 * e), c)
        mm("P%d" % (4 + h), 192, "qv", 0, "qx", c)
        act(V("YS", c, e), V("P%d" % (4 + h), 0, 192))
        dma("a", "y", T.y[:, c:e], T.YS[:, c:e], [V("YS", c, e)], [])
        dma("s", "out", T.oc[:, 4 * c:4 * e], T.qx[:, c:e].bitcast(dt.uint8), [V("qx", c, e)], [])
        for k in range(4):
            dma("s", "out", T.osc[4 * k:4 * k + 4, c:e], T.sqx[32 * k:32 * k + 4, c:e], [V("sqx", c, e)], [])
    act(V("OMB", 0, 384, 2), V("TT2", 384, 576))
    act(V("OMB", 1, 384, 2), V("TT2", 576, 768))
    act(V("OMB", 384, 768), V("TT2", 0, 384), 1.0, V("POS"))
    dma("s", "om", T.om[:], T.OMB[0::16, :], [V("OMB")], [])
    emit_all()
